import numpy as np, ml_dtypes
CORES = [2,3,42,43,82,83,122,123]
N = 8
import mx_ref
BF = ml_dtypes.bfloat16
def entries(a):
    return np.ascontiguousarray(a.T).reshape(-1)
def table(e):
    return np.ascontiguousarray(np.reshape(e, (-1, 16)).T).astype(np.int32)
def f(rng, *shape):
    return mx_ref.flush((rng.standard_normal(shape, dtype=np.float32) * np.exp2(rng.integers(-2, 3, shape[:-1] + (1,)))).astype(BF))
def wide(rng, *shape, cols=0):
    v = rng.standard_normal(shape, dtype=np.float32) * np.exp2(rng.integers(-12, 13, shape)).astype(np.float32)
    if cols: v *= np.repeat(np.exp2(rng.integers(-cols, cols + 1, shape[:-2] + (1, shape[-1] // 4))) * (rng.random(shape[:-2] + (1, shape[-1] // 4)) > 0.0625), 4, axis=-1).astype(np.float32)
    return mx_ref.flush(v.astype(BF))
T = 512
def listed(a):
    k = np.full((2 * N, 128), -1)
    for s in range(2 * N):
        i = np.flatnonzero(a == s); k[s, :len(i)] = i
    return k.reshape(-1)
def lists(rng, one=False, absent=False, sort=False, alike=False):
    t, a, k = [], [], []; nobody = rng.integers(0, N)
    for r in range(N):
        if r == 0 or not alike:
            u = np.concatenate([rng.permutation(8)[:2] for q in range(N)])
            if absent:
                here = rng.permutation([q for q in range(N) if q != nobody])[:T // 256 + r % 3].tolist()
                u.reshape(N, 2)[[q for q in range(N) if q not in here]] = -1
            else: u[rng.permutation(2 * N)[:rng.integers(0, 5)]] = -1
        v = rng.permutation(np.flatnonzero(u >= 0))
        if one: e = np.concatenate([np.full(128, v[0]), np.resize(v[1:], T - 128)])
        else:
            room = np.zeros(2 * N, int); room[v] = rng.integers(0, 129, len(v))
            for s in v:
                if room.sum() < T: room[s] = 128
            e = np.repeat(np.arange(2 * N), room)
        e = rng.permutation(e)[:T]
        if sort: e = np.sort(e)
        t.append(table(u)); a.append(table(e)); k.append(table(listed(e)))
    return {"tab": np.stack(t), "ad": np.stack(a), "tok": np.stack(k)}
def setup_inputs(rng):
    return {"x": f(rng, N, 128, 4 * T), "wa": f(rng, N, 1024, 512), **lists(rng)}
def setup_inputs_absent(rng):
    return {**setup_inputs(rng), **lists(rng, absent=True)}
def setup_inputs_alike(rng):
    return {**setup_inputs(rng), **lists(rng, alike=True)}
def setup_inputs_one(rng):
    return {**setup_inputs(rng), **lists(rng, one=True)}
def setup_inputs_sorted(rng):
    return {**setup_inputs(rng), **lists(rng, sort=True)}
def setup_inputs_spread(rng):
    d = setup_inputs(rng); d["x"] = wide(rng, N, 128, 4 * T, cols=8); return d
def check_inputs(d):
    b = []
    for n in ("x", "wa"):
        v = np.abs(np.asarray(d[n]).astype(np.float32))
        if not ((v == 0) | ((v >= 2.0 ** -30) & (v <= 2.0 ** 30))).all(): b.append(n)
    for r in range(N):
        u, a, k = entries(d["tab"][r]), entries(d["ad"][r]), entries(d["tok"][r]); p = u.reshape(N, 2)
        if u.min() < -1 or u.max() > 7 or ((p[:, 0] == p[:, 1]) & (p[:, 0] >= 0)).any(): b.append("tab")
        if a.min() < 0 or a.max() >= 2 * N or (u[a] < 0).any() or np.bincount(a).max() > 128: b.append("ad")
        elif (k != listed(a)).any(): b.append("tok")
    return b
def reference(x, wa, tab, ad, tok):
    y = np.zeros((N, 128, T), np.float32)
    for r in range(N):
        u, a, X = entries(tab[r]), entries(ad[r]), mx_ref.quantize(x[r])
        for s in range(2 * N):
            i = np.flatnonzero(a == s)
            if len(i) == 0: continue
            A = wa[s // 2][128 * u[s]:128 * u[s] + 128]
            y[r][:, i] = mx_ref.matmul(mx_ref.quantize(A), X)[:, i]
    return {"y": y}

@@ -1,0 +1,323 @@
+from concourse.bass import DstId, RemoteDMATransfer
+from concourse.mybir import dt, AluOpType as Op, ActivationFunctionType as Fn
+
+NB = 10
+NC = 128 * NB
+NAT = 6
+W0 = 512 * NAT
+SPLIT = 640
+XE = 2
+SE = 960
+PW = 1824
+
+SCRATCH = {n: ("sbuf", [128, w], d) for d, ws in {
+    "int32": {"tab1": 16, "tabb": 16, "tokS": 80, "adS": 32, "pidx": 4, "pi1": 4, "pi2": 4, "tokA": 80, "tokB": 80},
+    "bfloat16": {"tabf": 16, "win": 4096, "xs": 2048, "xg": 4 * NC, "ga": 8192},
+    "uint16": {"offa": 512, "offx": 80, "offs": 80, "offy": 32},
+    "float32": {"p16f": 4, "oddf": 4, "evf": 4, "odd16": 4, "iot": 80, "dumpc": 80, "negf": 80, "ndf": 80, "offf": 80,
+                "vals": NC, "posw": PW, "trp": 512, "f1": 32, "f2": 32, "f3": 32, "n1": 32, "n2": 32, "n3": 32, "n4": 32,
+                "tot": 32, "resw": W0 + NC, "ysb": 512},
+    "float8_e4m3fn_x4": {"qc": 2048, "lc": 2048, "xc": 512, "xgc": NC},
+    "uint8": {"qs": 2048, "ls": 2048, "xcs": 512, "xgs": NC},
+}.items() for n, w in ws.items()}
+SCRATCH["tabd"] = ("dram", [128, 1], "int32")
+SCRATCH["tabr"] = ("dram", [8, 128, 1], "int32")
+for _b in range(8):
+    SCRATCH["ps%d" % _b] = ("psum", [128, 512], "float32")
+SEMAPHORES = (["e%d" % _i for _i in range(120)] + ["a%d" % _i for _i in range(8)]
+              + ["dtab", "dtw", "dx", "dw", "dt", "da", "dy0", "dy1", "tabs", "tsent", "loc", "h0", "h1"])
+
+
+def _mask(es):
+    return sum(1 << e for e in es)
+
+
+def _road(r, T, topo):
+    cores = list(T.cores)
+    chips = []
+    for c in cores:
+        if topo.chip(c) not in chips:
+            chips.append(topo.chip(c))
+    mem = [[q for q in range(len(cores)) if topo.chip(cores[q]) == ch] for ch in chips]
+    me = cores[r]
+    k = chips.index(topo.chip(me))
+    h = mem[k].index(r)
+    rel = [mem[k ^ s][1 - h] for s in (1, 2, 3)]
+    dire = [mem[k ^ s][h] for s in (1, 2, 3)]
+    nb = mem[k][1 - h]
+    free = [c for c in topo.cores_of(me) if c not in cores]
+    port = [c for c in free if topo.die(c) != topo.die(me) and all(topo.may_write(c, cores[d]) for d in rel)]
+    far = [c for c in free if topo.die(c) != topo.die(me) and c not in port and topo.may_write(c, cores[rel[1]])]
+    near = [c for c in free if topo.die(c) == topo.die(me) and topo.may_write(c, cores[dire[1]])]
+    via = {rel[0]: port[h], rel[2]: port[h], rel[1]: far[h], dire[1]: near[h]}
+    off = topo.engines(me, cores[dire[0]])
+    on = [e for e in topo.engines(me, cores[nb]) if e not in off]
+    eng = {d: topo.engines(via.get(d, me), cores[d]) for d in rel + dire}
+    eng[nb] = on
+    tabe, left = {}, list(off)
+    for i, d in enumerate(rel + dire):
+        n = 2 if i < len(off) - len(rel + dire) else 1
+        tabe[d], left = left[:n], left[n:]
+    tabe[nb] = on
+    pairs = [rel[0], rel[1], dire[1], dire[0], rel[2], dire[2], nb, r]
+    return {"k": k, "h": h, "nb": nb, "via": via, "off": off, "on": on, "eng": eng, "tab": tabe, "pairs": pairs,
+            "order": [r, nb, rel[0], rel[1], dire[0], dire[1], rel[2], dire[2]]}
+
+
+def _tr(topo, dst, engines, sem, src, to):
+    rid, pid, _se = topo.addr(dst)
+    return RemoteDMATransfer(dst_ids=[DstId(rid=rid, pnc=pid)], dma_engine_mask=_mask(engines), remote_sem=sem, src=src, dst=to)
+
+
+def _send(g, T, topo, bufs, items):
+    n = 0
+    for c, (b, l) in zip((True, False), bufs):
+        ts = []
+        for a, w, dst, engines, sem, at in items:
+            src, to = T[b][:, a:a + w], T[l][:, at:at + w]
+            ts.append(_tr(topo, dst, engines, sem, src.bitcast(dt.uint8) if c else src, to.bitcast(dt.uint8) if c else to))
+            n += len(engines)
+        g.remote_dma_fused(ts, local_sem=T.sem.loc)
+    return n
+
+
+def _relay(g, core, r, R, T, topo):
+    n, i = 0, 0
+    for d in R["pairs"]:
+        if R["via"].get(d) == core:
+            g.wait_ge(T.sem["h%d" % i], 2 * len(R["on"]))
+            n += _send(g, T, topo, (("lc", "lc"), ("ls", "ls")),
+                       [(256 * i, 256, T.cores[d], R["eng"][d], T.sem["a%d" % r], 256 * r)])
+            i += 1
+    g.wait_ge(T.sem.loc, n)
+
+
+def rank_program(g, core, T, topo):
+    rank = T.rank_of(core)
+    cores = list(T.cores)
+    roads = [_road(q, T, topo) for q in range(len(cores))]
+    if rank is None:
+        for q, R in enumerate(roads):
+            if core in R["via"].values():
+                _relay(g, core, q, R, T, topo)
+        return
+    R = roads[rank]
+    V, S, P, Y = g.vector, g.scalar, g.tensor, g.sync
+    pairs = R["pairs"]
+    nat0 = 0 if R["k"] < 2 else 16 - NAT
+    listed = [s for s in range(16) if not nat0 <= s < nat0 + NAT]
+    c0 = 8 * listed[0]
+    used = [0]
+    waited = {}
+
+    def new():
+        used[0] += 1
+        return ["e%d" % (used[0] - 1), 0]
+
+    def sig(inst, e=None):
+        e = e or new()
+        inst.then_inc(T.sem[e[0]], 1)
+        e[1] += 1
+        return e
+
+    def need(qn, *es):
+        q = {"g": g, "V": V, "S": S, "P": P, "Y": Y}[qn]
+        for e in es:
+            if waited.get((qn, e[0]), 0) < e[1]:
+                q.wait_ge(T.sem[e[0]], e[1])
+                waited[(qn, e[0])] = e[1]
+
+    Y.dma_start(T.tabd[0:16, :], T.tab[:]).then_inc(T.sem.dtab, 16)
+    S.dma_start(T.tabd[16:128, :], T.tok[0:7, 0:16]).then_inc(T.sem.dtab, 16)
+    S.dma_start(T.tabr[rank, 0:16, :], T.tab[:]).then_inc(T.sem.dtab, 16)
+    for b in range(8):
+        (S if b < 4 else Y).dma_start(T.tokS[16 * b:16 * b + 16, :], T.tok[:, c0:c0 + 80]).then_inc(T.sem.dt, 16)
+    Y.dma_start(T.xs[:], T.x[:]).then_inc(T.sem.dx, 16)
+    for m in range(8):
+        if m == 4:
+            Y.wait_ge(T.sem.tsent, 1)
+        Y.dma_start(T.win[:, 512 * m:512 * m + 512], T.wa[128 * m:128 * m + 128, :]).then_inc(T.sem.dw, 16)
+    for b in range(8):
+        Y.dma_start(T.adS[16 * b:16 * b + 16, :], T.ad[:]).then_inc(T.sem.da, 16)
+
+    e_pidx = sig(g.iota(T.pidx[:, 0:1], [[0, 1]], 0, 1))
+    e_iot = sig(g.iota(T.iot[:], [[16, 80]], 17, 0, allow_small_or_imprecise_dtypes=True))
+    e_v0 = sig(g.iota(T.vals[:, 0:512], [[1, 512]], W0, 0, allow_small_or_imprecise_dtypes=True))
+    need("S", e_v0)
+    e_val = sig(S.activation(T.vals[:, 512:1024], T.vals[:, 0:512], Fn.Identity, bias=512.0))
+    sig(S.activation(T.vals[:, 1024:NC], T.vals[:, 0:NC - 1024], Fn.Identity, bias=1024.0), e_val)
+
+    g.wait_ge(T.sem.dtab, 48)
+    g.remote_dma_fused([_tr(topo, cores[d], R["tab"][d], T.sem.tabs, T.tabd[:], T.tabr[rank]) for d in pairs[:7]],
+                       local_sem=T.sem.loc)
+    nloc = sum(len(R["tab"][d]) for d in pairs[:7])
+    g.sem_inc(T.sem.tsent, 1)
+
+    Y.wait_ge(T.sem.dtab, 48)
+    Y.wait_ge(T.sem.tabs, sum(len(roads[q]["tab"][rank]) for q in range(len(cores)) if q != rank))
+    Y.dma_start(T.tab1[0:1, 0:16], T.tabr[:, 2 * rank:2 * rank + 2, 0]).then_inc(T.sem.dtw, 16)
+    g.wait_ge(T.sem.dtw, 16)
+    e_pb = sig(g.partition_broadcast(T.tabb[:], T.tab1[0:1, 0:16], 128))
+
+    need("V", e_pidx)
+    e1 = sig(V.tensor_scalar(T.pi1[:, 0:1], T.pidx[:, 0:1], 15, None, Op.bitwise_and))
+    e2 = sig(V.tensor_scalar(T.pi2[:, 0:1], T.pidx[:, 0:1], 4, 1, Op.logical_shift_right, Op.bitwise_and))
+    need("V", e1, e2)
+    e_p16 = sig(V.tensor_copy(T.p16f[:, 0:1], T.pi1[:, 0:1]))
+    e_c = sig(V.tensor_copy(T.oddf[:, 0:1], T.pi2[:, 0:1]))
+    sig(V.tensor_scalar(T.odd16[:, 0:1], T.pi2[:, 0:1], 16.0, None, Op.mult), e_c)
+    sig(V.tensor_scalar(T.evf[:, 0:1], T.pi2[:, 0:1], -1.0, 1.0, Op.mult, Op.add), e_c)
+    need("V", e_iot, e_p16)
+    sig(V.tensor_scalar(T.dumpc[:], T.iot[:], T.p16f[:, 0:1], None, Op.add), e_c)
+    e_pz = sig(V.memset(T.posw[:, 0:512], 0.0))
+
+    V.wait_ge(T.sem.dt, 128)
+    e_ox = sig(V.tensor_scalar(T.offx[:], T.tokS[:], 0.0, 4.0, Op.max, Op.mult))
+    need("V", e_c)
+    e3 = sig(V.tensor_scalar(T.tokA[:], T.tokS[:], T.odd16[:, 0:1], None, Op.subtract))
+    e4 = sig(V.tensor_scalar(T.negf[:], T.tokS[:], 0.0, None, Op.is_lt))
+    need("V", e3)
+    e5 = sig(V.tensor_scalar(T.tokB[:], T.tokA[:], 511, None, Op.bitwise_and))
+    need("V", e4)
+    e6 = sig(V.tensor_tensor(T.ndf[:], T.negf[:], T.dumpc[:], Op.mult))
+    need("V", e5, e6)
+    e7 = sig(V.tensor_tensor(T.offf[:], T.ndf[:], T.tokB[:], Op.add))
+    need("V", e7)
+    e8 = sig(V.tensor_copy(T.offs[:], T.offf[:]))
+    need("V", e8, e_val, e_pz)
+    e_sc = new()
+
+    def scatter(a, b):
+        if a < b:
+            sig(V.tensor_copy(T.posw[:].indirect(T.offs[:, a // 16:b // 16]), T.vals[:, a:b]), e_sc)
+
+    scatter(0, SE)
+    V.wait_ge(T.sem.dx, 16)
+    e_xq = sig(V.quantize_mx(T.xc[:], T.xcs[:], T.xs[:]))
+
+    e_xg = new()
+
+    def xgather(t):
+        sig(S.activation(T.xg[:, t:4 * NC:4], T.xs[:, t:2048].indirect(T.offx[:]), Fn.Copy), e_xg)
+
+    S.wait_ge(T.sem.dx, 16)
+    need("S", e_ox)
+    for t in range(XE):
+        xgather(t)
+
+    need("V", e_pb)
+    e_tab = sig(V.tensor_scalar(T.tabf[:], T.tabb[:], 0.0, 512.0, Op.max, Op.mult))
+    need("V", e_tab)
+    e_off = {}
+
+    def offsets(i):
+        if i < 8:
+            d, e = pairs[i], new()
+            for j in range(2):
+                sig(V.tensor_scalar(T.offa[:, 64 * i + 32 * j:64 * i + 32 * j + 32], T.dumpc[:, 0:32],
+                                    T.tabf[:, 2 * d + j:2 * d + j + 1], -17.0, Op.add, Op.add), e)
+            e_off[i] = e
+
+    offsets(0)
+    offsets(1)
+    V.wait_ge(T.sem.dw, 128)
+    S.wait_ge(T.sem.dw, 128)
+    e_q = []
+    for i in range(8):
+        a, m = 1024 * i, SPLIT // 16
+        need("S", e_off[i])
+        es = sig(S.activation(T.ga[:, a:a + SPLIT], T.win[:].indirect(T.offa[:, 64 * i:64 * i + m]), Fn.Copy))
+        need("V", e_off[i])
+        ev = sig(V.tensor_copy(T.ga[:, a + SPLIT:a + 1024], T.win[:].indirect(T.offa[:, 64 * i + m:64 * i + 64])))
+        offsets(i + 2)
+        need("V", es, ev)
+        e_q.append(sig(V.quantize_mx(T.qc[:, 256 * i:256 * i + 256], T.qs[:, 256 * i:256 * i + 256], T.ga[:, a:a + 1024])))
+    for t in range(XE, 4):
+        xgather(t)
+    scatter(SE, NC)
+
+    bufs, held = (("qc", "lc"), ("qs", "ls")), {}
+
+    def item(i):
+        d = pairs[i]
+        c = R["via"].get(d)
+        if c is None:
+            return (256 * i, 256, cores[d], R["eng"][d], T.sem["a%d" % rank], 256 * rank)
+        held[c] = held.get(c, -1) + 1
+        return (256 * i, 256, c, R["on"], T.sem["h%d" % held[c]], 256 * held[c])
+
+    for group in ((0, 1), (2, 3), (4, 5), (6,)):
+        need("g", *[e_q[i] for i in group])
+        items = [item(i) for i in group]
+        if group == (0, 1):
+            items = [it[:3] + (es,) + it[4:] for it, es in zip(items, (R["off"], R["on"]))]
+        nloc += _send(g, T, topo, bufs, items)
+    g.wait_ge(T.sem.loc, nloc)
+
+    need("V", e_sc)
+    e_t = sig(V.transpose(T.trp[:], T.posw[:, 0:512]))
+    V.wait_ge(T.sem.da, 128)
+    if nat0 == 0:
+        n1 = sig(V.tensor_scalar(T.n1[:], T.adS[:], NAT - 0.5, None, Op.is_lt))
+    else:
+        n1 = sig(V.tensor_scalar(T.n1[:], T.adS[:], nat0 - 0.5, None, Op.is_gt))
+    n2 = sig(V.tensor_scalar(T.n2[:], T.adS[:], 512.0, -512.0 * nat0 - 17.0, Op.mult, Op.add))
+    need("V", e_t)
+    f = sig(V.tensor_scalar(T.f1[:], T.trp[:, 0:512:16], T.evf[:, 0:1], None, Op.mult))
+    sig(V.tensor_scalar(T.f2[:, 1:32], T.trp[:, 0:496:16], T.oddf[:, 0:1], None, Op.mult), f)
+    sig(V.tensor_scalar(T.f2[:, 0:1], T.trp[:, 496:497], T.oddf[:, 0:1], None, Op.mult), f)
+    need("V", n2)
+    n3 = sig(V.tensor_tensor(T.n3[:], T.n2[:], T.dumpc[:, 0:32], Op.add))
+    need("V", f)
+    f3 = sig(V.tensor_tensor(T.f3[:], T.f1[:], T.f2[:], Op.add))
+    need("V", n1, n3)
+    n4 = sig(V.tensor_tensor(T.n4[:], T.n3[:], T.n1[:], Op.mult))
+    need("V", n4, f3)
+    tt = sig(V.tensor_tensor(T.tot[:], T.n4[:], T.f3[:], Op.add))
+    need("V", tt)
+    e_oy = sig(V.tensor_copy(T.offy[:], T.tot[:]))
+    need("V", e_xg)
+    e_gq = []
+    for a, b in ((0, 512), (512, 1024), (1024, NC)):
+        e_gq.append(sig(V.quantize_mx(T.xgc[:, a:b], T.xgs[:, a:b], T.xg[:, 4 * a:4 * b])))
+
+    copies, n = [], 0
+    for src in R["order"]:
+        if src == rank:
+            need("P", e_q[7])
+            cb, sb, at = T.qc, T.qs, 256 * 7
+        else:
+            P.wait_ge(T.sem["a%d" % src], 2 * len(roads[src]["eng"][rank]))
+            cb, sb, at = T.lc, T.ls, 256 * src
+        for j in range(2):
+            s, b = 2 * src + j, T["ps%d" % (n % 8)]
+            if n >= 8:
+                need("P", copies[n - 8])
+            if s in listed:
+                x0, w, xa, xb = 128 * listed.index(s), 128, T.xgc, T.xgs
+                need("P", e_gq[x0 // 512])
+                out = W0 + x0
+            else:
+                x0, w, xa, xb = 0, 512, T.xc, T.xcs
+                need("P", e_xq)
+                out = 512 * (s - nat0)
+            e = sig(P.matmul_mx(b[:, 0:w], cb[:, at + 128 * j:at + 128 * j + 128], sb[:, at + 128 * j:at + 128 * j + 128],
+                                xa[:, x0:x0 + w], xb[:, x0:x0 + w], True, True))
+            if j == 0:
+                need("S", e)
+                copies.append(sig(S.activation(T.resw[:, out:out + w], b[:, 0:w], Fn.Copy)))
+            else:
+                need("V", e)
+                copies.append(sig(V.tensor_copy(T.resw[:, out:out + w], b[:, 0:w])))
+            n += 1
+
+    need("V", e_oy, *copies)
+    e_y = sig(V.tensor_copy(T.ysb[:, 0:256], T.resw[:].indirect(T.offy[:, 0:16])))
+    need("S", e_oy, *copies)
+    e_z = sig(S.activation(T.ysb[:, 256:512], T.resw[:].indirect(T.offy[:, 16:32]), Fn.Copy))
+    need("Y", e_y)
+    Y.dma_start(T.y[:, 0:256], T.ysb[:, 0:256]).then_inc(T.sem.dy0, 16)
+    need("S", e_z)
+    S.dma_start(T.y[:, 256:512], T.ysb[:, 256:512]).then_inc(T.sem.dy1, 16)
+    Y.wait_ge(T.sem.dy0, 16)
+    S.wait_ge(T.sem.dy1, 16)

@@ -1,22 +1,39 @@
-from concourse.bass import DstId, RemoteDMATransfer
+from concourse.bass import DstId, RemoteDMATransfer, IndirectOffsetOnAxis
 from concourse.mybir import dt, AluOpType as Op, ActivationFunctionType as Fn
 
 NB = 10
 NC = 128 * NB
 NAT = 6
 W0 = 512 * NAT
-SPLIT = 640
-XE = 2
-SE = 960
-PW = 1824
+QE = NC // 4
+PT = 544
+CFG = {
+    "split": 704,
+    "gate": 4,
+    "rows": 2,
+    "pairs": ["ring", "other", "ring0", "plane0", "other0", "plane1", "nb"],
+    "calls": [[(k,) + t for t in group] for group in (
+        [(0, 1, "mate1", "off", 1, 0), (1, 1, "port", "on", 1, 0)],
+        [(2, 1, "mate0", "off", 1, 0), (3, 1, "near", "on", 1, 0)],
+        [(4, 1, None, "off", 1, 0), (5, 1, "far", "on", 1, 0)],
+        [(6, 1, None, "on", 1, 0)]) for k in "cs"],
+    "relay": {v: [[(k, i, 1, 0)] for k in "cs"] for v, i in (("mate1", 0), ("port", 1), ("mate0", 2), ("near", 3), ("far", 5))},
+    "order": ["me", "nb", "other", "ring", "plane0", "plane1", "other0", "ring0"],
+    "early": ["ramp", "offx", "c", "qoff", "xq", "neg", "i0", "nd", "idx", "o1", "a1", "offs", "a2", "scat"],
+    "fill": [["t1"], ["t2"], [], [], [], [], [], ["turn"]],
+    "xS": ([(0, 1024, 0), (0, 1024, 1)], [(0, 512, 2), (512, NC, 2), (1024, NC, 0), (1024, NC, 1)]),
+    "xV": ["u", (0, 512, 3), "c1", (512, NC, 3), "m1", (0, 512), "c2", (512, 1024), "m2", (1024, NC), "offy"],
+    "copyV": (3, 5, 7, 9, 11, 13, 15),
+}
 
 SCRATCH = {n: ("sbuf", [128, w], d) for d, ws in {
-    "int32": {"tab1": 16, "tabb": 16, "tokS": 80, "adS": 32, "pidx": 4, "pi1": 4, "pi2": 4, "tokA": 80, "tokB": 80},
-    "bfloat16": {"tabf": 16, "win": 4096, "xs": 2048, "xg": 4 * NC, "ga": 8192},
-    "uint16": {"offa": 512, "offx": 80, "offs": 80, "offy": 32},
-    "float32": {"p16f": 4, "oddf": 4, "evf": 4, "odd16": 4, "iot": 80, "dumpc": 80, "negf": 80, "ndf": 80, "offf": 80,
-                "vals": NC, "posw": PW, "trp": 512, "f1": 32, "f2": 32, "f3": 32, "n1": 32, "n2": 32, "n3": 32, "n4": 32,
-                "tot": 32, "resw": W0 + NC, "ysb": 512},
+    "int32": {"tabo": 16, "tabb": 16, "tabc": 4, "tokS": 128, "adS": 32, "pidx": 4, "pi1": 4, "pi2": 4, "pi3": 4, "q1": 4,
+              "q2": 4, "a1": 32, "a2": 32, "idx": 4},
+    "bfloat16": {"rep": 32, "tabf": 32, "win": 4096, "xs": 2048, "xg": 4 * NC, "ga": 8192},
+    "uint16": {"offa": 512, "offx": 80, "offs": 32, "offy": 32, "qoff": 4, "pick": 4, "zero": 4},
+    "float32": {"p16": 4, "pf": 4, "ev16": 4, "b20": 4, "bq": 4, "i0": 4, "iot": 32, "ramp": 32, "dump": 32, "neg": 32, "nd": 32,
+                "o1": 32, "val0": QE, "vals": QE, "posw": PT + 544, "trp": PT, "t1": 32, "t2": 32, "u": 32, "c1": 32,
+                "m1": 32, "c2": 32, "m2": 32, "resw": W0 + NC, "ysb": 512},
     "float8_e4m3fn_x4": {"qc": 2048, "lc": 2048, "xc": 512, "xgc": NC},
     "uint8": {"qs": 2048, "ls": 2048, "xcs": 512, "xgs": NC},
 }.items() for n, w in ws.items()}
@@ -24,44 +41,57 @@ SCRATCH["tabd"] = ("dram", [128, 1], "int32")
 SCRATCH["tabr"] = ("dram", [8, 128, 1], "int32")
 for _b in range(8):
     SCRATCH["ps%d" % _b] = ("psum", [128, 512], "float32")
-SEMAPHORES = (["e%d" % _i for _i in range(120)] + ["a%d" % _i for _i in range(8)]
-              + ["dtab", "dtw", "dx", "dw", "dt", "da", "dy0", "dy1", "tabs", "tsent", "loc", "h0", "h1"])
+SEMAPHORES = (["e%d" % _i for _i in range(124)] + ["a%d" % _i for _i in range(8)] + ["h%d" % _i for _i in range(4)]
+              + ["dtab", "down", "dtw", "dx", "dw", "dt", "da", "dy0", "dy1", "tabs", "tsent", "loc", "dto", "drow"])
+BUFS = {"c": ("qc", "lc"), "s": ("qs", "ls")}
+ALL_CORES = 128
 
 
 def _mask(es):
     return sum(1 << e for e in es)
 
 
+def _part(es, parts, k):
+    n = len(es) // parts
+    return es[n * k:n * k + n]
+
+
 def _road(r, T, topo):
     cores = list(T.cores)
-    chips = []
-    for c in cores:
-        if topo.chip(c) not in chips:
-            chips.append(topo.chip(c))
-    mem = [[q for q in range(len(cores)) if topo.chip(cores[q]) == ch] for ch in chips]
+    n = len(cores)
     me = cores[r]
-    k = chips.index(topo.chip(me))
-    h = mem[k].index(r)
-    rel = [mem[k ^ s][1 - h] for s in (1, 2, 3)]
-    dire = [mem[k ^ s][h] for s in (1, 2, 3)]
-    nb = mem[k][1 - h]
+    on_chip = [q for q in range(n) if topo.chip(cores[q]) == topo.chip(me)]
+    h = on_chip.index(r)
+    nb = on_chip[1 - h]
+    step = r - nb
+    who = {"me": r, "nb": nb, "ring": (r + step) % n, "ring0": (r + 2 * step) % n, "plane1": (r + 3 * step) % n,
+           "plane0": (r + 4 * step) % n, "other": (r + 5 * step) % n, "other0": (r + 6 * step) % n}
+    pairs = [who[d] for d in CFG["pairs"]]
     free = [c for c in topo.cores_of(me) if c not in cores]
-    port = [c for c in free if topo.die(c) != topo.die(me) and all(topo.may_write(c, cores[d]) for d in rel)]
-    far = [c for c in free if topo.die(c) != topo.die(me) and c not in port and topo.may_write(c, cores[rel[1]])]
-    near = [c for c in free if topo.die(c) == topo.die(me) and topo.may_write(c, cores[dire[1]])]
-    via = {rel[0]: port[h], rel[2]: port[h], rel[1]: far[h], dire[1]: near[h]}
-    off = topo.engines(me, cores[dire[0]])
-    on = [e for e in topo.engines(me, cores[nb]) if e not in off]
-    eng = {d: topo.engines(via.get(d, me), cores[d]) for d in rel + dire}
-    eng[nb] = on
-    tabe, left = {}, list(off)
-    for i, d in enumerate(rel + dire):
-        n = 2 if i < len(off) - len(rel + dire) else 1
-        tabe[d], left = left[:n], left[n:]
-    tabe[nb] = on
-    pairs = [rel[0], rel[1], dire[1], dire[0], rel[2], dire[2], nb, r]
-    return {"k": k, "h": h, "nb": nb, "via": via, "off": off, "on": on, "eng": eng, "tab": tabe, "pairs": pairs,
-            "order": [r, nb, rel[0], rel[1], dire[0], dire[1], rel[2], dire[2]]}
+    port = [c for c in free if topo.die(c) != topo.die(me) and topo.may_write(c, cores[who["ring"]])]
+    relay = {"port": port[h], "far": [c for c in free if topo.die(c) != topo.die(me) and c not in port][h],
+             "near": [c for c in free if topo.die(c) == topo.die(me)][h]}
+    for v, cs in CFG["relay"].items():
+        if v not in relay:
+            d = cores[pairs[cs[0][0][1]]]
+            mate = [c for c in range(ALL_CORES) if topo.chip(c) != topo.chip(d) and topo.mates(topo.chip(c), topo.chip(d))
+                    and topo.may_write(c, d) and (topo.die(c) == topo.die(d)) == (v == "mate0")]
+            relay[v] = mate[[c for c in cores if topo.chip(c) == topo.chip(d)].index(d)]
+    off = topo.engines(me, cores[who["ring"]])
+    every = topo.engines(me, cores[nb])
+    eng = {"off": off, "all": every, "on": [e for e in every if e not in off]}
+    away = [q for q in range(n) if q not in on_chip]
+    tab = {d: [off[i]] for i, d in enumerate(away)}
+    tab[nb] = eng["on"][:1]
+    calls = [[(k, i, m, to, _part(eng[e], parts, part)) for k, i, m, to, e, parts, part in call] for call in CFG["calls"]]
+    onward = {v: [[(k, i, _part(topo.engines(relay[v], cores[pairs[i]]), parts, part)) for k, i, parts, part in call]
+                  for call in cs] for v, cs in CFG["relay"].items()}
+    lands = {d: 0 for d in pairs}
+    for k, i, m, to, es in sum(calls, []):
+        lands[pairs[i]] += len(es) if to is None else 0
+    for k, i, es in sum(sum(onward.values(), []), []):
+        lands[pairs[i]] += len(es)
+    return {"who": who, "pairs": pairs, "tab": tab, "relay": relay, "calls": calls, "onward": onward, "lands": lands}
 
 
 def _tr(topo, dst, engines, sem, src, to):
@@ -69,44 +99,43 @@ def _tr(topo, dst, engines, sem, src, to):
     return RemoteDMATransfer(dst_ids=[DstId(rid=rid, pnc=pid)], dma_engine_mask=_mask(engines), remote_sem=sem, src=src, dst=to)
 
 
-def _send(g, T, topo, bufs, items):
-    n = 0
-    for c, (b, l) in zip((True, False), bufs):
-        ts = []
-        for a, w, dst, engines, sem, at in items:
-            src, to = T[b][:, a:a + w], T[l][:, at:at + w]
-            ts.append(_tr(topo, dst, engines, sem, src.bitcast(dt.uint8) if c else src, to.bitcast(dt.uint8) if c else to))
-            n += len(engines)
-        g.remote_dma_fused(ts, local_sem=T.sem.loc)
-    return n
+def _run(T, name, a, w):
+    v = T[name][:, a:a + w]
+    return v.bitcast(dt.uint8) if name in BUFS["c"] else v
 
 
-def _relay(g, core, r, R, T, topo):
-    n, i = 0, 0
-    for d in R["pairs"]:
-        if R["via"].get(d) == core:
-            g.wait_ge(T.sem["h%d" % i], 2 * len(R["on"]))
-            n += _send(g, T, topo, (("lc", "lc"), ("ls", "ls")),
-                       [(256 * i, 256, T.cores[d], R["eng"][d], T.sem["a%d" % r], 256 * r)])
-            i += 1
+def _relay(g, v, r, R, T, topo):
+    got = [(k, i, m, es) for k, i, m, to, es in sum(R["calls"], []) if to == v]
+    n, seen = 0, set()
+    for call in R["onward"][v]:
+        for k, i, _es in call:
+            j = [j for j, (k0, i0, m, _e) in enumerate(got) if k0 == k and i0 <= i < i0 + m][0]
+            if j not in seen:
+                g.wait_ge(T.sem["h%d" % j], len(got[j][3]))
+                seen.add(j)
+        g.remote_dma_fused([_tr(topo, T.cores[R["pairs"][i]], es, T.sem["a%d" % r], _run(T, BUFS[k][1], 256 * i, 256),
+                                _run(T, BUFS[k][1], 256 * r, 256)) for k, i, es in call], local_sem=T.sem.loc)
+        n += sum(len(es) for _k, _i, es in call)
     g.wait_ge(T.sem.loc, n)
 
 
 def rank_program(g, core, T, topo):
     rank = T.rank_of(core)
     cores = list(T.cores)
-    roads = [_road(q, T, topo) for q in range(len(cores))]
+    N = len(cores)
+    roads = [_road(q, T, topo) for q in range(N)]
     if rank is None:
         for q, R in enumerate(roads):
-            if core in R["via"].values():
-                _relay(g, core, q, R, T, topo)
+            for v in R["onward"]:
+                if R["relay"][v] == core:
+                    _relay(g, v, q, R, T, topo)
         return
     R = roads[rank]
     V, S, P, Y = g.vector, g.scalar, g.tensor, g.sync
-    pairs = R["pairs"]
-    nat0 = 0 if R["k"] < 2 else 16 - NAT
-    listed = [s for s in range(16) if not nat0 <= s < nat0 + NAT]
-    c0 = 8 * listed[0]
+    pairs = R["pairs"] + [rank]
+    rows = CFG["rows"]
+    nat0 = 2 * (rank - 1) % 16
+    c0 = 8 * ((nat0 + NAT) % 16)
     used = [0]
     waited = {}
 
@@ -129,93 +158,133 @@ def rank_program(g, core, T, topo):
 
     Y.dma_start(T.tabd[0:16, :], T.tab[:]).then_inc(T.sem.dtab, 16)
     S.dma_start(T.tabd[16:128, :], T.tok[0:7, 0:16]).then_inc(T.sem.dtab, 16)
-    S.dma_start(T.tabr[rank, 0:16, :], T.tab[:]).then_inc(T.sem.dtab, 16)
     for b in range(8):
-        (S if b < 4 else Y).dma_start(T.tokS[16 * b:16 * b + 16, :], T.tok[:, c0:c0 + 80]).then_inc(T.sem.dt, 16)
+        (S if b < 4 else Y).dma_start(T.tokS[16 * b:16 * b + 16, :], T.tok[:]).then_inc(T.sem.dt, 16)
     Y.dma_start(T.xs[:], T.x[:]).then_inc(T.sem.dx, 16)
+    if rows:
+        S.dma_start(T.tabo[0:1, 0:16], T.tab[:]).then_inc(T.sem.dto, 16)
+    for b in range(2):
+        S.dma_start(T.adS[16 * b:16 * b + 16, :], T.ad[:]).then_inc(T.sem.da, 16)
+    S.dma_start(T.tabr[rank, 0:16, :], T.tab[:]).then_inc(T.sem.down, 16)
     for m in range(8):
-        if m == 4:
+        if m == CFG["gate"]:
             Y.wait_ge(T.sem.tsent, 1)
         Y.dma_start(T.win[:, 512 * m:512 * m + 512], T.wa[128 * m:128 * m + 128, :]).then_inc(T.sem.dw, 16)
-    for b in range(8):
-        Y.dma_start(T.adS[16 * b:16 * b + 16, :], T.ad[:]).then_inc(T.sem.da, 16)
 
     e_pidx = sig(g.iota(T.pidx[:, 0:1], [[0, 1]], 0, 1))
-    e_iot = sig(g.iota(T.iot[:], [[16, 80]], 17, 0, allow_small_or_imprecise_dtypes=True))
-    e_v0 = sig(g.iota(T.vals[:, 0:512], [[1, 512]], W0, 0, allow_small_or_imprecise_dtypes=True))
-    need("S", e_v0)
-    e_val = sig(S.activation(T.vals[:, 512:1024], T.vals[:, 0:512], Fn.Identity, bias=512.0))
-    sig(S.activation(T.vals[:, 1024:NC], T.vals[:, 0:NC - 1024], Fn.Identity, bias=1024.0), e_val)
-
-    g.wait_ge(T.sem.dtab, 48)
+    e_iot = sig(g.iota(T.iot[:], [[16, 32]], 0, 0, allow_small_or_imprecise_dtypes=True))
+    e_v0 = sig(g.iota(T.val0[:], [[1, QE]], W0, 0, allow_small_or_imprecise_dtypes=True))
+    g.wait_ge(T.sem.dtab, 32)
     g.remote_dma_fused([_tr(topo, cores[d], R["tab"][d], T.sem.tabs, T.tabd[:], T.tabr[rank]) for d in pairs[:7]],
                        local_sem=T.sem.loc)
     nloc = sum(len(R["tab"][d]) for d in pairs[:7])
     g.sem_inc(T.sem.tsent, 1)
+    ev = {"dt": ["dt", 128], "da": ["da", 32], "dx": ["dx", 16]}
+    if rows:
+        g.wait_ge(T.sem.dto, 16)
+        ev["pb"] = sig(g.partition_broadcast(T.tabb[:], T.tabo[0:1, 0:16], 128))
 
-    Y.wait_ge(T.sem.dtab, 48)
-    Y.wait_ge(T.sem.tabs, sum(len(roads[q]["tab"][rank]) for q in range(len(cores)) if q != rank))
-    Y.dma_start(T.tab1[0:1, 0:16], T.tabr[:, 2 * rank:2 * rank + 2, 0]).then_inc(T.sem.dtw, 16)
-    g.wait_ge(T.sem.dtw, 16)
-    e_pb = sig(g.partition_broadcast(T.tabb[:], T.tab1[0:1, 0:16], 128))
-
+    e_z = sig(V.memset(T.tabc[:], 0))
+    ev["z"] = sig(V.memset(T.posw[:, 0:PT], 0.0))
     need("V", e_pidx)
     e1 = sig(V.tensor_scalar(T.pi1[:, 0:1], T.pidx[:, 0:1], 15, None, Op.bitwise_and))
-    e2 = sig(V.tensor_scalar(T.pi2[:, 0:1], T.pidx[:, 0:1], 4, 1, Op.logical_shift_right, Op.bitwise_and))
-    need("V", e1, e2)
-    e_p16 = sig(V.tensor_copy(T.p16f[:, 0:1], T.pi1[:, 0:1]))
-    e_c = sig(V.tensor_copy(T.oddf[:, 0:1], T.pi2[:, 0:1]))
-    sig(V.tensor_scalar(T.odd16[:, 0:1], T.pi2[:, 0:1], 16.0, None, Op.mult), e_c)
-    sig(V.tensor_scalar(T.evf[:, 0:1], T.pi2[:, 0:1], -1.0, 1.0, Op.mult, Op.add), e_c)
-    need("V", e_iot, e_p16)
-    sig(V.tensor_scalar(T.dumpc[:], T.iot[:], T.p16f[:, 0:1], None, Op.add), e_c)
-    e_pz = sig(V.memset(T.posw[:, 0:512], 0.0))
+    sig(V.tensor_scalar(T.pi2[:, 0:1], T.pidx[:, 0:1], 16, None, Op.bitwise_and), e1)
+    sig(V.tensor_scalar(T.pi3[:, 0:1], T.pidx[:, 0:1], 5, None, Op.logical_shift_right), e1)
+    sig(V.memset(T.t2[:], 0.0), ev["z"])
+    sig(V.memset(T.zero[:], 0), ev["z"])
+    e2 = sig(V.tensor_copy(T.pf[:, 0:1], T.pidx[:, 0:1]))
+    need("V", e1)
+    sig(V.tensor_copy(T.p16[:, 0:1], T.pi1[:, 0:1]), e2)
+    sig(V.tensor_scalar(T.b20[:, 0:1], T.pi3[:, 0:1], QE / 16.0, float(c0), Op.mult, Op.add), e2)
+    sig(V.tensor_scalar(T.ev16[:, 0:1], T.pi2[:, 0:1], -1.0, 16.0, Op.mult, Op.add), e2)
+    e_bq = sig(V.tensor_scalar(T.bq[:, 0:1], T.pi3[:, 0:1], float(QE), None, Op.mult))
+    ev.update(iot=e_iot, col=e2)
+    need("S", e_v0, e_bq)
+    ev["val"] = sig(S.activation(T.vals[:], T.val0[:], Fn.Identity, bias=T.bq[:, 0:1]))
 
-    V.wait_ge(T.sem.dt, 128)
-    e_ox = sig(V.tensor_scalar(T.offx[:], T.tokS[:], 0.0, 4.0, Op.max, Op.mult))
-    need("V", e_c)
-    e3 = sig(V.tensor_scalar(T.tokA[:], T.tokS[:], T.odd16[:, 0:1], None, Op.subtract))
-    e4 = sig(V.tensor_scalar(T.negf[:], T.tokS[:], 0.0, None, Op.is_lt))
-    need("V", e3)
-    e5 = sig(V.tensor_scalar(T.tokB[:], T.tokA[:], 511, None, Op.bitwise_and))
-    need("V", e4)
-    e6 = sig(V.tensor_tensor(T.ndf[:], T.negf[:], T.dumpc[:], Op.mult))
-    need("V", e5, e6)
-    e7 = sig(V.tensor_tensor(T.offf[:], T.ndf[:], T.tokB[:], Op.add))
-    need("V", e7)
-    e8 = sig(V.tensor_copy(T.offs[:], T.offf[:]))
-    need("V", e8, e_val, e_pz)
-    e_sc = new()
+    Y.wait_ge(T.sem.down, 16)
+    need("Y", e_z)
+    Y.wait_ge(T.sem.tabs, sum(len(roads[q]["tab"][rank]) for q in range(N) if q != rank))
+    for b in range(4):
+        Y.dma_start(T.tabc[32 * b:32 * b + 16, 0:1], T.tabr[:, 2 * rank:2 * rank + 2, 0]).then_inc(T.sem.dtw, 16)
 
-    def scatter(a, b):
-        if a < b:
-            sig(V.tensor_copy(T.posw[:].indirect(T.offs[:, a // 16:b // 16]), T.vals[:, a:b]), e_sc)
+    cut = min(80, 128 - c0)
+    quarter = T.tokS[:].indirect(T.qoff[:, 0:2])
+    steps = {
+        "ramp": (["iot", "col"], lambda: [
+            V.tensor_scalar(T.q1[:, 0:2], T.iot[:, 0:2], T.p16[:, 0:1], T.b20[:, 0:1], Op.add, Op.add),
+            V.tensor_scalar(T.ramp[:], T.iot[:], T.p16[:, 0:1], None, Op.add),
+            V.tensor_scalar(T.dump[:], T.iot[:], T.p16[:, 0:1], PT + 1.0, Op.add, Op.add)]),
+        "c": (["ramp"], lambda: [V.tensor_scalar(T.q2[:, 0:2], T.q1[:, 0:2], 127, None, Op.bitwise_and),
+                                 V.tensor_scalar(T.pick[:, 0:2], T.ramp[:, 0:2], 16.0, T.ev16[:, 0:1], Op.mult, Op.add)]),
+        "qoff": (["c"], lambda: [V.tensor_copy(T.qoff[:, 0:2], T.q2[:, 0:2])]),
+        "offx": (["dt"], lambda: [
+            V.tensor_scalar(T.offx[:, a:b], T.tokS[:, (c0 + a) % 128:(c0 + a) % 128 + b - a], 0.0, 4.0, Op.max, Op.mult)
+            for a, b in ((0, cut), (cut, 80)) if a < b]),
+        "xq": (["dx"], lambda: [V.quantize_mx(T.xc[:], T.xcs[:], T.xs[:])]),
+        "i0": (["pb"], lambda: [V.tensor_scalar(T.i0[:, 0:2], T.tabb[:, 2 * rank:2 * rank + 2], 0.0, 128.0, Op.max, Op.mult)]),
+        "idx": (["i0"], lambda: [V.tensor_scalar(T.idx[:, 0:2], T.i0[:, 0:2], T.pf[:, 0:1], None, Op.add)]),
+        "neg": (["dt", "qoff"], lambda: [V.tensor_scalar(T.neg[:], quarter, 0.0, None, Op.is_lt)]),
+        "nd": (["neg"], lambda: [V.tensor_tensor(T.nd[:], T.neg[:], T.dump[:], Op.mult)]),
+        "o1": (["nd"], lambda: [V.tensor_tensor(T.o1[:], quarter, T.nd[:], Op.add)]),
+        "offs": (["o1"], lambda: [V.tensor_scalar(T.offs[:], T.o1[:], T.ev16[:, 0:1], None, Op.add)]),
+        "scat": (["offs", "val", "z"], lambda: [V.tensor_copy(T.posw[:].indirect(T.offs[:, 0:QE // 16]), T.vals[:])]),
+        "turn": (["scat"], lambda: [V.transpose(T.trp[:], T.posw[:, 0:PT])]),
+        "a1": (["da"], lambda: [V.tensor_scalar(T.a1[0:32, :], T.adS[0:32, :], 16.0 - nat0, None, Op.add)]),
+        "a2": (["a1"], lambda: [V.tensor_scalar(T.a2[0:32, :], T.a1[0:32, :], 15, None, Op.bitwise_and)]),
+        "t1": (["a2"], lambda: [V.tensor_scalar(T.t1[0:32, :], T.a2[0:32, :], -512.0, 512.0 * (NAT - 1), Op.mult, Op.add)]),
+        "t2": (["t1", "z"], lambda: [V.tensor_tensor(T.t2[0:32, :], T.t1[0:32, :], T.ramp[0:32, :], Op.add)]),
+        "u": (["turn", "t2", "c"], lambda: [V.tensor_tensor(T.u[:], T.trp[:].indirect(T.pick[:, 0:2]), T.t2[:], Op.max)]),
+        "c1": (["u"], lambda: [V.tensor_copy(T.c1[0:64, :], T.u[64:128, :])]),
+        "m1": (["c1"], lambda: [V.tensor_tensor(T.m1[0:64, :], T.u[0:64, :], T.c1[0:64, :], Op.max)]),
+        "c2": (["m1"], lambda: [V.tensor_copy(T.c2[0:32, :], T.m1[32:64, :])]),
+        "m2": (["c2"], lambda: [V.tensor_tensor(T.m2[0:32, :], T.m1[0:32, :], T.c2[0:32, :], Op.max)]),
+        "offy": (["m2"], lambda: [V.tensor_copy(T.offy[32 * b:32 * b + 32, :], T.m2[0:32, :]) for b in range(4)]),
+    }
+    e_xg, e_gq = [], []
 
-    scatter(0, SE)
-    V.wait_ge(T.sem.dx, 16)
-    e_xq = sig(V.quantize_mx(T.xc[:], T.xcs[:], T.xs[:]))
+    def work(qn, jobs):
+        for job in jobs:
+            if job in steps:
+                if rows or job not in ("i0", "idx"):
+                    need("V", *[ev[d] for d in steps[job][0]])
+                    ev[job] = new()
+                    for inst in steps[job][1]():
+                        sig(inst, ev[job])
+                continue
+            a, b = job[:2] if R["who"]["nb"] > rank else (NC - job[1], NC - job[0])
+            if len(job) == 2:
+                need("V", *[e for a0, b0, e in e_xg if a0 < b and a < b0])
+                e_gq.append((a, b, sig(V.quantize_mx(T.xgc[:, a:b], T.xgs[:, a:b], T.xg[:, 4 * a:4 * b]))))
+                continue
+            t = job[2]
+            need(qn, ev["dx"], ev["offx"])
+            out, src = T.xg[:, 4 * a + t:4 * b:4], T.xs[:, t:2048].indirect(T.offx[:, a // 16:b // 16])
+            e_xg.append((a, b, sig(S.activation(out, src, Fn.Copy) if qn == "S" else V.tensor_copy(out, src))))
 
-    e_xg = new()
+    work("V", CFG["early"])
+    work("S", CFG["xS"][0])
+    if rows:
+        need("g", ev["idx"])
+        for j in range(2 - rows, 2):
+            g.indirect_dma_start(T.ga[:, 7168 + 512 * j:7680 + 512 * j], None, T.wa[:],
+                                 IndirectOffsetOnAxis(ap=T.idx[:, j:j + 1], axis=0), bounds_check=1023).then_inc(T.sem.drow, 16)
 
-    def xgather(t):
-        sig(S.activation(T.xg[:, t:4 * NC:4], T.xs[:, t:2048].indirect(T.offx[:]), Fn.Copy), e_xg)
-
-    S.wait_ge(T.sem.dx, 16)
-    need("S", e_ox)
-    for t in range(XE):
-        xgather(t)
-
-    need("V", e_pb)
-    e_tab = sig(V.tensor_scalar(T.tabf[:], T.tabb[:], 0.0, 512.0, Op.max, Op.mult))
-    need("V", e_tab)
+    V.wait_ge(T.sem.dtw, 64)
+    need("V", e_z, ev["z"])
+    e = sig(V.tensor_scalar(T.rep[:], T.tabc[:].indirect(T.zero[:, 0:2]), 0.0, 512.0, Op.max, Op.mult))
+    need("V", e)
+    e = sig(V.transpose(T.tabf[:], T.rep[:]))
+    need("V", e)
     e_off = {}
+    width = [1024] * 7 + [1024 - 512 * rows]
 
     def offsets(i):
-        if i < 8:
+        if i < 8 and width[i]:
             d, e = pairs[i], new()
-            for j in range(2):
-                sig(V.tensor_scalar(T.offa[:, 64 * i + 32 * j:64 * i + 32 * j + 32], T.dumpc[:, 0:32],
-                                    T.tabf[:, 2 * d + j:2 * d + j + 1], -17.0, Op.add, Op.add), e)
+            for j in range(width[i] // 512):
+                sig(V.tensor_scalar(T.offa[:, 64 * i + 32 * j:64 * i + 32 * j + 32], T.ramp[:],
+                                    T.tabf[:, 2 * d + j:2 * d + j + 1], None, Op.add), e)
             e_off[i] = e
 
     offsets(0)
@@ -224,96 +293,71 @@ def rank_program(g, core, T, topo):
     S.wait_ge(T.sem.dw, 128)
     e_q = []
     for i in range(8):
-        a, m = 1024 * i, SPLIT // 16
-        need("S", e_off[i])
-        es = sig(S.activation(T.ga[:, a:a + SPLIT], T.win[:].indirect(T.offa[:, 64 * i:64 * i + m]), Fn.Copy))
-        need("V", e_off[i])
-        ev = sig(V.tensor_copy(T.ga[:, a + SPLIT:a + 1024], T.win[:].indirect(T.offa[:, 64 * i + m:64 * i + 64])))
-        offsets(i + 2)
-        need("V", es, ev)
+        a, sp, both = 1024 * i, CFG["split"] * width[i] // 1024, []
+        if width[i]:
+            m, n = sp // 16, width[i] // 16
+            need("S", e_off[i])
+            both.append(sig(S.activation(T.ga[:, a:a + sp], T.win[:].indirect(T.offa[:, 64 * i:64 * i + m]), Fn.Copy)))
+            need("V", e_off[i])
+            both.append(sig(V.tensor_copy(T.ga[:, a + sp:a + width[i]], T.win[:].indirect(T.offa[:, 64 * i + m:64 * i + n]))))
+            offsets(i + 2)
+        work("V", CFG["fill"][i])
+        need("V", *both)
+        if i == 7 and rows:
+            V.wait_ge(T.sem.drow, 16 * rows)
         e_q.append(sig(V.quantize_mx(T.qc[:, 256 * i:256 * i + 256], T.qs[:, 256 * i:256 * i + 256], T.ga[:, a:a + 1024])))
-    for t in range(XE, 4):
-        xgather(t)
-    scatter(SE, NC)
+    work("S", CFG["xS"][1])
+    work("V", CFG["xV"])
 
-    bufs, held = (("qc", "lc"), ("qs", "ls")), {}
-
-    def item(i):
-        d = pairs[i]
-        c = R["via"].get(d)
-        if c is None:
-            return (256 * i, 256, cores[d], R["eng"][d], T.sem["a%d" % rank], 256 * rank)
-        held[c] = held.get(c, -1) + 1
-        return (256 * i, 256, c, R["on"], T.sem["h%d" % held[c]], 256 * held[c])
-
-    for group in ((0, 1), (2, 3), (4, 5), (6,)):
-        need("g", *[e_q[i] for i in group])
-        items = [item(i) for i in group]
-        if group == (0, 1):
-            items = [it[:3] + (es,) + it[4:] for it, es in zip(items, (R["off"], R["on"]))]
-        nloc += _send(g, T, topo, bufs, items)
+    held = {}
+    for call in R["calls"]:
+        ts = []
+        for k, i, m, to, es in call:
+            need("g", *e_q[i:i + m])
+            if to is None:
+                dst, at, sem = cores[pairs[i]], 256 * rank, "a%d" % rank
+            else:
+                held[to] = held.get(to, -1) + 1
+                dst, at, sem = R["relay"][to], 256 * i, "h%d" % held[to]
+            ts.append(_tr(topo, dst, es, T.sem[sem], _run(T, BUFS[k][0], 256 * i, 256 * m), _run(T, BUFS[k][1], at, 256 * m)))
+            nloc += len(es)
+        g.remote_dma_fused(ts, local_sem=T.sem.loc)
     g.wait_ge(T.sem.loc, nloc)
 
-    need("V", e_sc)
-    e_t = sig(V.transpose(T.trp[:], T.posw[:, 0:512]))
-    V.wait_ge(T.sem.da, 128)
-    if nat0 == 0:
-        n1 = sig(V.tensor_scalar(T.n1[:], T.adS[:], NAT - 0.5, None, Op.is_lt))
-    else:
-        n1 = sig(V.tensor_scalar(T.n1[:], T.adS[:], nat0 - 0.5, None, Op.is_gt))
-    n2 = sig(V.tensor_scalar(T.n2[:], T.adS[:], 512.0, -512.0 * nat0 - 17.0, Op.mult, Op.add))
-    need("V", e_t)
-    f = sig(V.tensor_scalar(T.f1[:], T.trp[:, 0:512:16], T.evf[:, 0:1], None, Op.mult))
-    sig(V.tensor_scalar(T.f2[:, 1:32], T.trp[:, 0:496:16], T.oddf[:, 0:1], None, Op.mult), f)
-    sig(V.tensor_scalar(T.f2[:, 0:1], T.trp[:, 496:497], T.oddf[:, 0:1], None, Op.mult), f)
-    need("V", n2)
-    n3 = sig(V.tensor_tensor(T.n3[:], T.n2[:], T.dumpc[:, 0:32], Op.add))
-    need("V", f)
-    f3 = sig(V.tensor_tensor(T.f3[:], T.f1[:], T.f2[:], Op.add))
-    need("V", n1, n3)
-    n4 = sig(V.tensor_tensor(T.n4[:], T.n3[:], T.n1[:], Op.mult))
-    need("V", n4, f3)
-    tt = sig(V.tensor_tensor(T.tot[:], T.n4[:], T.f3[:], Op.add))
-    need("V", tt)
-    e_oy = sig(V.tensor_copy(T.offy[:], T.tot[:]))
-    need("V", e_xg)
-    e_gq = []
-    for a, b in ((0, 512), (512, 1024), (1024, NC)):
-        e_gq.append(sig(V.quantize_mx(T.xgc[:, a:b], T.xgs[:, a:b], T.xg[:, 4 * a:4 * b])))
-
-    copies, n = [], 0
-    for src in R["order"]:
+    copies, last, n = [], {}, 0
+    sender = {d: q for q in range(N) for d in roads[q]["who"] if roads[q]["who"][d] == rank}
+    for name in CFG["order"]:
+        src = sender[name]
         if src == rank:
             need("P", e_q[7])
             cb, sb, at = T.qc, T.qs, 256 * 7
         else:
-            P.wait_ge(T.sem["a%d" % src], 2 * len(roads[src]["eng"][rank]))
+            P.wait_ge(T.sem["a%d" % src], roads[src]["lands"][rank])
             cb, sb, at = T.lc, T.ls, 256 * src
         for j in range(2):
-            s, b = 2 * src + j, T["ps%d" % (n % 8)]
+            s, b = (2 * src + j - nat0) % 16, T["ps%d" % (n % 8)]
             if n >= 8:
                 need("P", copies[n - 8])
-            if s in listed:
-                x0, w, xa, xb = 128 * listed.index(s), 128, T.xgc, T.xgs
-                need("P", e_gq[x0 // 512])
+            if s >= NAT:
+                x0, w, xa, xb = 128 * (s - NAT), 128, T.xgc, T.xgs
+                need("P", *[e for a, b0, e in e_gq if a <= x0 < b0])
                 out = W0 + x0
             else:
                 x0, w, xa, xb = 0, 512, T.xc, T.xcs
-                need("P", e_xq)
-                out = 512 * (s - nat0)
+                need("P", ev["xq"])
+                out = 512 * (NAT - 1 - s)
             e = sig(P.matmul_mx(b[:, 0:w], cb[:, at + 128 * j:at + 128 * j + 128], sb[:, at + 128 * j:at + 128 * j + 128],
                                 xa[:, x0:x0 + w], xb[:, x0:x0 + w], True, True))
-            if j == 0:
-                need("S", e)
-                copies.append(sig(S.activation(T.resw[:, out:out + w], b[:, 0:w], Fn.Copy)))
-            else:
-                need("V", e)
-                copies.append(sig(V.tensor_copy(T.resw[:, out:out + w], b[:, 0:w])))
+            qn = "V" if n in CFG["copyV"] else "S"
+            need(qn, e)
+            copies.append(sig(V.tensor_copy(T.resw[:, out:out + w], b[:, 0:w]) if qn == "V"
+                              else S.activation(T.resw[:, out:out + w], b[:, 0:w], Fn.Copy)))
+            last[qn] = copies[-1]
             n += 1
 
-    need("V", e_oy, *copies)
+    need("V", ev["offy"], last["V"], last["S"])
     e_y = sig(V.tensor_copy(T.ysb[:, 0:256], T.resw[:].indirect(T.offy[:, 0:16])))
-    need("S", e_oy, *copies)
+    need("S", ev["offy"], last["S"], last["V"])
     e_z = sig(S.activation(T.ysb[:, 256:512], T.resw[:].indirect(T.offy[:, 16:32]), Fn.Copy))
     need("Y", e_y)
     Y.dma_start(T.y[:, 0:256], T.ysb[:, 0:256]).then_inc(T.sem.dy0, 16)

@@ -8,31 +8,28 @@ W0 = 512 * NAT
 QE = NC // 4
 PT = 544
 CFG = {
-    "split": 704,
-    "gate": 4,
+    "split": [704, 672, 704, 672, 672, 608, 608, 0],
+    "gate": (3, 6),
     "rows": 2,
-    "pairs": ["ring", "other", "ring0", "plane0", "other0", "plane1", "nb"],
-    "calls": [[(k,) + t for t in group] for group in (
-        [(0, 1, "mate1", "off", 1, 0), (1, 1, "port", "on", 1, 0)],
-        [(2, 1, "mate0", "off", 1, 0), (3, 1, "near", "on", 1, 0)],
-        [(4, 1, None, "off", 1, 0), (5, 1, "far", "on", 1, 0)],
-        [(6, 1, None, "on", 1, 0)]) for k in "cs"],
-    "relay": {v: [[(k, i, 1, 0)] for k in "cs"] for v, i in (("mate1", 0), ("port", 1), ("mate0", 2), ("near", 3), ("far", 5))},
-    "order": ["me", "nb", "other", "ring", "plane0", "plane1", "other0", "ring0"],
-    "early": ["ramp", "offx", "c", "qoff", "xq", "neg", "i0", "nd", "idx", "o1", "a1", "offs", "a2", "scat"],
-    "fill": [["t1"], ["t2"], [], [], [], [], [], ["turn"]],
-    "xS": ([(0, 1024, 0), (0, 1024, 1)], [(0, 512, 2), (512, NC, 2), (1024, NC, 0), (1024, NC, 1)]),
-    "xV": ["u", (0, 512, 3), "c1", (512, NC, 3), "m1", (0, 512), "c2", (512, 1024), "m2", (1024, NC), "offy"],
+    "groups": 2 * [[[("other", ["far", "mate0"]), ("ring", ["port"])], [("other0", ["mate1"]), ("plane0", ["near"])],
+                    [("ring0", []), ("plane1", ["far"])], [("nb", [])]]],
+    "first": 4 * ["sc"], "fine": "sc", "turns": True, "lag": 1,
+    "order": 2 * [["me", "ring", "nb", "other0", "plane1", "other", "plane0", "ring0"]],
+    "early": ["offx", "nd", "ramp", "o1", "c", "offs", "i0", "xq", "idx", "scat", "a1"],
+    "fill": [[], [], [], [], [], ["a2"], ["t1"], ["t2", "turn"]],
+    "xS": ([(0, 1024, 0), (0, 1024, 1)], [(0, 512, 2), (512, 1024, 2)] + [(1024, NC, _t) for _t in range(4)]),
+    "xV": ["u", (0, 512, 3), "c1", (512, 1024, 3), "m1", (0, 512), "c2", (512, 1024), "m2", (1024, NC), "offy"],
     "copyV": (3, 5, 7, 9, 11, 13, 15),
+    "tail": [("V", 0, 256, "Y"), ("S", 256, 512, "S")],
 }
 
 SCRATCH = {n: ("sbuf", [128, w], d) for d, ws in {
-    "int32": {"tabo": 16, "tabb": 16, "tabc": 4, "tokS": 128, "adS": 32, "pidx": 4, "pi1": 4, "pi2": 4, "pi3": 4, "q1": 4,
+    "int32": {"tabo": 16, "tabb": 16, "tabc": 4, "tokS": 80, "adS": 32, "pidx": 4, "pi1": 4, "pi2": 4, "pi3": 4, "q1": 4,
               "q2": 4, "a1": 32, "a2": 32, "idx": 4},
     "bfloat16": {"rep": 32, "tabf": 32, "win": 4096, "xs": 2048, "xg": 4 * NC, "ga": 8192},
     "uint16": {"offa": 512, "offx": 80, "offs": 32, "offy": 32, "qoff": 4, "pick": 4, "zero": 4},
-    "float32": {"p16": 4, "pf": 4, "ev16": 4, "b20": 4, "bq": 4, "i0": 4, "iot": 32, "ramp": 32, "dump": 32, "neg": 32, "nd": 32,
-                "o1": 32, "val0": QE, "vals": QE, "posw": PT + 544, "trp": PT, "t1": 32, "t2": 32, "u": 32, "c1": 32,
+    "float32": {"p16": 4, "pf": 4, "ev16": 4, "b20": 4, "bq": 4, "bq4": 4, "i0": 4, "iot": QE // 4, "ramp": 32, "dump": 80, "nd": 80,
+                "o1": 80, "vals": QE, "posw": PT + 8 * QE + 16, "trp": PT, "t1": 32, "t2": 32, "u": 32, "c1": 32,
                 "m1": 32, "c2": 32, "m2": 32, "resw": W0 + NC, "ysb": 512},
     "float8_e4m3fn_x4": {"qc": 2048, "lc": 2048, "xc": 512, "xgc": NC},
     "uint8": {"qs": 2048, "ls": 2048, "xcs": 512, "xgs": NC},
@@ -41,9 +38,10 @@ SCRATCH["tabd"] = ("dram", [128, 1], "int32")
 SCRATCH["tabr"] = ("dram", [8, 128, 1], "int32")
 for _b in range(8):
     SCRATCH["ps%d" % _b] = ("psum", [128, 512], "float32")
-SEMAPHORES = (["e%d" % _i for _i in range(124)] + ["a%d" % _i for _i in range(8)] + ["h%d" % _i for _i in range(4)]
+SEMAPHORES = (["e%d" % _i for _i in range(126)] + ["a%d" % _i for _i in range(8)]
               + ["dtab", "down", "dtw", "dx", "dw", "dt", "da", "dy0", "dy1", "tabs", "tsent", "loc", "dto", "drow"])
 BUFS = {"c": ("qc", "lc"), "s": ("qs", "ls")}
+PIECES = {"s": (BUFS["s"], 0, 256), "c": (BUFS["c"], 0, 256), "a": (BUFS["c"], 0, 128), "b": (BUFS["c"], 128, 128)}
 ALL_CORES = 128
 
 
@@ -66,32 +64,42 @@ def _road(r, T, topo):
     step = r - nb
     who = {"me": r, "nb": nb, "ring": (r + step) % n, "ring0": (r + 2 * step) % n, "plane1": (r + 3 * step) % n,
            "plane0": (r + 4 * step) % n, "other": (r + 5 * step) % n, "other0": (r + 6 * step) % n}
-    pairs = [who[d] for d in CFG["pairs"]]
+    groups = CFG["groups"][h]
+    pairs = [who[d] for grp in groups for d, _way in grp]
     free = [c for c in topo.cores_of(me) if c not in cores]
     port = [c for c in free if topo.die(c) != topo.die(me) and topo.may_write(c, cores[who["ring"]])]
-    relay = {"port": port[h], "far": [c for c in free if topo.die(c) != topo.die(me) and c not in port][h],
+    local = {"port": port[h], "far": [c for c in free if topo.die(c) != topo.die(me) and c not in port][h],
              "near": [c for c in free if topo.die(c) == topo.die(me)][h]}
-    for v, cs in CFG["relay"].items():
-        if v not in relay:
-            d = cores[pairs[cs[0][0][1]]]
-            mate = [c for c in range(ALL_CORES) if topo.chip(c) != topo.chip(d) and topo.mates(topo.chip(c), topo.chip(d))
-                    and topo.may_write(c, d) and (topo.die(c) == topo.die(d)) == (v == "mate0")]
-            relay[v] = mate[[c for c in cores if topo.chip(c) == topo.chip(d)].index(d)]
+
+    def relay(v, d):
+        if v in local:
+            return local[v]
+        k, hd = int(v[-1]), [c for c in cores if topo.chip(c) == topo.chip(d)].index(d)
+        return [c for c in range(ALL_CORES) if topo.chip(c) != topo.chip(d) and topo.mates(topo.chip(c), topo.chip(d))
+                and topo.may_write(c, d) and topo.die(c) == ((k + hd) % 2 if CFG["turns"] else k)][k if CFG["turns"] else hd]
+
     off = topo.engines(me, cores[who["ring"]])
     every = topo.engines(me, cores[nb])
-    eng = {"off": off, "all": every, "on": [e for e in every if e not in off]}
+    on = [e for e in every if e not in off]
     away = [q for q in range(n) if q not in on_chip]
     tab = {d: [off[i]] for i, d in enumerate(away)}
-    tab[nb] = eng["on"][:1]
-    calls = [[(k, i, m, to, _part(eng[e], parts, part)) for k, i, m, to, e, parts, part in call] for call in CFG["calls"]]
-    onward = {v: [[(k, i, _part(topo.engines(relay[v], cores[pairs[i]]), parts, part)) for k, i, parts, part in call]
-                  for call in cs] for v, cs in CFG["relay"].items()}
-    lands = {d: 0 for d in pairs}
-    for k, i, m, to, es in sum(calls, []):
-        lands[pairs[i]] += len(es) if to is None else 0
-    for k, i, es in sum(sum(onward.values(), []), []):
-        lands[pairs[i]] += len(es)
-    return {"who": who, "pairs": pairs, "tab": tab, "relay": relay, "calls": calls, "onward": onward, "lands": lands}
+    tab[nb] = on[:1]
+    road = [[me] + [relay(v, cores[who[d]]) for v in way] + [cores[who[d]]] for grp in groups for d, way in grp]
+    calls, i = [], 0
+    for grp in groups:
+        ids, i = range(i, i + len(grp)), i + len(grp)
+        out = [j for j in ids if topo.chip(road[j][1]) != topo.chip(me)]
+        stay = [j for j in ids if j not in out]
+        calls.append([(j, _part(off, len(out), out.index(j))) for j in out]
+                     + [(j, _part(on if out or ids[0] else every, len(stay), stay.index(j))) for j in stay])
+    hops = {}
+    for j, es in sum(calls, []):
+        hops[j, 0] = es
+        for a in range(1, len(road[j]) - 1):
+            hops[j, a] = topo.engines(road[j][a], road[j][a + 1])
+    first = [ks for grp, ks in zip(groups, CFG["first"]) for _d in grp]
+    pieces = {(j, a): CFG["fine"] if a and len(road[j]) > 3 else first[j] for j, a in hops}
+    return {"who": who, "h": h, "pieces": pieces, "pairs": pairs, "tab": tab, "road": road, "calls": calls, "hops": hops}
 
 
 def _tr(topo, dst, engines, sem, src, to):
@@ -104,19 +112,28 @@ def _run(T, name, a, w):
     return v.bitcast(dt.uint8) if name in BUFS["c"] else v
 
 
-def _relay(g, v, r, R, T, topo):
-    got = [(k, i, m, es) for k, i, m, to, es in sum(R["calls"], []) if to == v]
-    n, seen = 0, set()
-    for call in R["onward"][v]:
-        for k, i, _es in call:
-            j = [j for j, (k0, i0, m, _e) in enumerate(got) if k0 == k and i0 <= i < i0 + m][0]
-            if j not in seen:
-                g.wait_ge(T.sem["h%d" % j], len(got[j][3]))
-                seen.add(j)
-        g.remote_dma_fused([_tr(topo, T.cores[R["pairs"][i]], es, T.sem["a%d" % r], _run(T, BUFS[k][1], 256 * i, 256),
-                                _run(T, BUFS[k][1], 256 * r, 256)) for k, i, es in call], local_sem=T.sem.loc)
-        n += sum(len(es) for _k, _i, es in call)
-    g.wait_ge(T.sem.loc, n)
+def _held(k, i):
+    return "e%d" % (len(PIECES) * i + list(PIECES).index(k))
+
+
+def _hop(T, topo, r, R, i, a, k):
+    last = a + 2 == len(R["road"][i])
+    bufs, o, w = PIECES[k]
+    return _tr(topo, R["road"][i][a + 1], R["hops"][i, a], T.sem["a%d" % r if last else _held(k, i)],
+               _run(T, bufs[min(a, 1)], 256 * i + o, w), _run(T, bufs[1], 256 * (r if last else i) + o, w))
+
+
+def _relay(g, core, r, R, T, topo):
+    n = 0
+    for i, road in enumerate(R["road"]):
+        if core in road[1:-1]:
+            a = road.index(core)
+            for k in R["pieces"][i, a]:
+                g.wait_ge(T.sem[_held(k if k in R["pieces"][i, a - 1] else "c", i)], len(R["hops"][i, a - 1]))
+                g.remote_dma_fused([_hop(T, topo, r, R, i, a, k)], local_sem=T.sem.loc)
+                n += len(R["hops"][i, a])
+    if n:
+        g.wait_ge(T.sem.loc, n)
 
 
 def rank_program(g, core, T, topo):
@@ -126,9 +143,7 @@ def rank_program(g, core, T, topo):
     roads = [_road(q, T, topo) for q in range(N)]
     if rank is None:
         for q, R in enumerate(roads):
-            for v in R["onward"]:
-                if R["relay"][v] == core:
-                    _relay(g, v, q, R, T, topo)
+            _relay(g, core, q, R, T, topo)
         return
     R = roads[rank]
     V, S, P, Y = g.vector, g.scalar, g.tensor, g.sync
@@ -158,77 +173,81 @@ def rank_program(g, core, T, topo):
 
     Y.dma_start(T.tabd[0:16, :], T.tab[:]).then_inc(T.sem.dtab, 16)
     S.dma_start(T.tabd[16:128, :], T.tok[0:7, 0:16]).then_inc(T.sem.dtab, 16)
-    for b in range(8):
-        (S if b < 4 else Y).dma_start(T.tokS[16 * b:16 * b + 16, :], T.tok[:]).then_inc(T.sem.dt, 16)
+    cut, w = min(80, 128 - c0), QE // 16
+    runs = [(a, z) for a, z in ((0, cut), (cut, 80)) if a < z]
+    for b, q in enumerate((S, Y)):
+        for a, z in runs:
+            q.dma_start(T.tokS[16 * b:16 * b + 16, a:z], T.tok[:, (c0 + a) % 128:(c0 + a) % 128 + z - a]).then_inc(T.sem.dt, 16)
     Y.dma_start(T.xs[:], T.x[:]).then_inc(T.sem.dx, 16)
     if rows:
         S.dma_start(T.tabo[0:1, 0:16], T.tab[:]).then_inc(T.sem.dto, 16)
     for b in range(2):
         S.dma_start(T.adS[16 * b:16 * b + 16, :], T.ad[:]).then_inc(T.sem.da, 16)
     S.dma_start(T.tabr[rank, 0:16, :], T.tab[:]).then_inc(T.sem.down, 16)
-    for m in range(8):
-        if m == CFG["gate"]:
-            Y.wait_ge(T.sem.tsent, 1)
-        Y.dma_start(T.win[:, 512 * m:512 * m + 512], T.wa[128 * m:128 * m + 128, :]).then_inc(T.sem.dw, 16)
+
+    def load(ms):
+        for m in ms:
+            Y.dma_start(T.win[:, 512 * m:512 * m + 512], T.wa[128 * m:128 * m + 128, :]).then_inc(T.sem.dw, 16)
+
+    load(range(CFG["gate"][0]))
+    Y.wait_ge(T.sem.tsent, 1)
+    load(range(*CFG["gate"]))
 
     e_pidx = sig(g.iota(T.pidx[:, 0:1], [[0, 1]], 0, 1))
-    e_iot = sig(g.iota(T.iot[:], [[16, 32]], 0, 0, allow_small_or_imprecise_dtypes=True))
-    e_v0 = sig(g.iota(T.val0[:], [[1, QE]], W0, 0, allow_small_or_imprecise_dtypes=True))
+    e_dump = sig(g.iota(T.dump[0:32, :], [[-32, 80]], -PT, -1, allow_small_or_imprecise_dtypes=True))
+    e_iot = sig(g.iota(T.iot[:], [[1, QE // 4]], 0, 0, allow_small_or_imprecise_dtypes=True))
     g.wait_ge(T.sem.dtab, 32)
     g.remote_dma_fused([_tr(topo, cores[d], R["tab"][d], T.sem.tabs, T.tabd[:], T.tabr[rank]) for d in pairs[:7]],
                        local_sem=T.sem.loc)
     nloc = sum(len(R["tab"][d]) for d in pairs[:7])
     g.sem_inc(T.sem.tsent, 1)
-    ev = {"dt": ["dt", 128], "da": ["da", 32], "dx": ["dx", 16]}
+    ev = {"dt": ["dt", 32 * len(runs)], "da": ["da", 32], "dx": ["dx", 16]}
     if rows:
         g.wait_ge(T.sem.dto, 16)
         ev["pb"] = sig(g.partition_broadcast(T.tabb[:], T.tabo[0:1, 0:16], 128))
 
     e_z = sig(V.memset(T.tabc[:], 0))
-    ev["z"] = sig(V.memset(T.posw[:, 0:PT], 0.0))
+    ev["z"] = sig(V.memset(T.t2[:], 0.0))
+    sig(V.memset(T.zero[:], 0), ev["z"])
     need("V", e_pidx)
     e1 = sig(V.tensor_scalar(T.pi1[:, 0:1], T.pidx[:, 0:1], 15, None, Op.bitwise_and))
     sig(V.tensor_scalar(T.pi2[:, 0:1], T.pidx[:, 0:1], 16, None, Op.bitwise_and), e1)
     sig(V.tensor_scalar(T.pi3[:, 0:1], T.pidx[:, 0:1], 5, None, Op.logical_shift_right), e1)
-    sig(V.memset(T.t2[:], 0.0), ev["z"])
-    sig(V.memset(T.zero[:], 0), ev["z"])
     e2 = sig(V.tensor_copy(T.pf[:, 0:1], T.pidx[:, 0:1]))
+    ev["clear"] = sig(V.memset(T.posw[:, 0:PT // 2], 0.0))
     need("V", e1)
+    e_bq = sig(V.tensor_scalar(T.bq[:, 0:1], T.pi3[:, 0:1], float(QE), float(W0), Op.mult, Op.add))
     sig(V.tensor_copy(T.p16[:, 0:1], T.pi1[:, 0:1]), e2)
-    sig(V.tensor_scalar(T.b20[:, 0:1], T.pi3[:, 0:1], QE / 16.0, float(c0), Op.mult, Op.add), e2)
     sig(V.tensor_scalar(T.ev16[:, 0:1], T.pi2[:, 0:1], -1.0, 16.0, Op.mult, Op.add), e2)
-    e_bq = sig(V.tensor_scalar(T.bq[:, 0:1], T.pi3[:, 0:1], float(QE), None, Op.mult))
-    ev.update(iot=e_iot, col=e2)
-    need("S", e_v0, e_bq)
-    ev["val"] = sig(S.activation(T.vals[:], T.val0[:], Fn.Identity, bias=T.bq[:, 0:1]))
+    ev.update(iot=e_iot, col=e2, dump=e_dump)
+    need("V", e_iot, e_bq)
+    need("S", sig(V.tensor_scalar(T.bq4[:], T.iot[:, 0:4], 80.0, T.bq[:, 0:1], Op.mult, Op.add)))
+    ev["val"] = new()
+    for a in range(4):
+        sig(S.activation(T.vals[:, 80 * a:80 * a + 80], T.iot[:], Fn.Identity, bias=T.bq4[:, a:a + 1]), ev["val"])
+    need("S", ev["dx"])
+    ev["clear2"] = sig(S.activation(T.posw[:, PT // 2:PT], T.xs[:, 0:PT // 2], Fn.Identity, scale=0.0))
 
     Y.wait_ge(T.sem.down, 16)
     need("Y", e_z)
     Y.wait_ge(T.sem.tabs, sum(len(roads[q]["tab"][rank]) for q in range(N) if q != rank))
     for b in range(4):
         Y.dma_start(T.tabc[32 * b:32 * b + 16, 0:1], T.tabr[:, 2 * rank:2 * rank + 2, 0]).then_inc(T.sem.dtw, 16)
+    load(range(CFG["gate"][1], 8))
 
-    cut = min(80, 128 - c0)
-    quarter = T.tokS[:].indirect(T.qoff[:, 0:2])
     steps = {
-        "ramp": (["iot", "col"], lambda: [
-            V.tensor_scalar(T.q1[:, 0:2], T.iot[:, 0:2], T.p16[:, 0:1], T.b20[:, 0:1], Op.add, Op.add),
-            V.tensor_scalar(T.ramp[:], T.iot[:], T.p16[:, 0:1], None, Op.add),
-            V.tensor_scalar(T.dump[:], T.iot[:], T.p16[:, 0:1], PT + 1.0, Op.add, Op.add)]),
-        "c": (["ramp"], lambda: [V.tensor_scalar(T.q2[:, 0:2], T.q1[:, 0:2], 127, None, Op.bitwise_and),
-                                 V.tensor_scalar(T.pick[:, 0:2], T.ramp[:, 0:2], 16.0, T.ev16[:, 0:1], Op.mult, Op.add)]),
-        "qoff": (["c"], lambda: [V.tensor_copy(T.qoff[:, 0:2], T.q2[:, 0:2])]),
-        "offx": (["dt"], lambda: [
-            V.tensor_scalar(T.offx[:, a:b], T.tokS[:, (c0 + a) % 128:(c0 + a) % 128 + b - a], 0.0, 4.0, Op.max, Op.mult)
-            for a, b in ((0, cut), (cut, 80)) if a < b]),
+        "ramp": (["iot", "col"], lambda: [V.tensor_scalar(T.ramp[:], T.iot[:, 0:32], 16.0, T.p16[:, 0:1], Op.mult, Op.add)]),
+        "c": (["ramp"], lambda: [V.tensor_scalar(T.pick[:, 0:2], T.ramp[:, 0:2], 16.0, T.ev16[:, 0:1], Op.mult, Op.add)]),
+        "offx": (["dt"], lambda: [V.tensor_scalar(T.offx[32 * b:32 * b + 32, :], T.tokS[0:32, :], 0.0, 4.0, Op.max, Op.mult)
+                                  for b in range(4)]),
         "xq": (["dx"], lambda: [V.quantize_mx(T.xc[:], T.xcs[:], T.xs[:])]),
         "i0": (["pb"], lambda: [V.tensor_scalar(T.i0[:, 0:2], T.tabb[:, 2 * rank:2 * rank + 2], 0.0, 128.0, Op.max, Op.mult)]),
         "idx": (["i0"], lambda: [V.tensor_scalar(T.idx[:, 0:2], T.i0[:, 0:2], T.pf[:, 0:1], None, Op.add)]),
-        "neg": (["dt", "qoff"], lambda: [V.tensor_scalar(T.neg[:], quarter, 0.0, None, Op.is_lt)]),
-        "nd": (["neg"], lambda: [V.tensor_tensor(T.nd[:], T.neg[:], T.dump[:], Op.mult)]),
-        "o1": (["nd"], lambda: [V.tensor_tensor(T.o1[:], quarter, T.nd[:], Op.add)]),
-        "offs": (["o1"], lambda: [V.tensor_scalar(T.offs[:], T.o1[:], T.ev16[:, 0:1], None, Op.add)]),
-        "scat": (["offs", "val", "z"], lambda: [V.tensor_copy(T.posw[:].indirect(T.offs[:, 0:QE // 16]), T.vals[:])]),
+        "nd": (["dt", "dump"], lambda: [V.tensor_tensor(T.nd[0:32, :], T.tokS[0:32, :], T.dump[0:32, :], Op.mult)]),
+        "o1": (["nd"], lambda: [V.tensor_tensor(T.o1[0:32, :], T.tokS[0:32, :], T.nd[0:32, :], Op.max)]),
+        "offs": (["o1", "col"], lambda: [V.tensor_scalar(T.offs[32 * b:32 * b + 32, 0:w], T.o1[0:32, w * b:w * b + w],
+                                                         T.ev16[0:32, 0:1], None, Op.add) for b in range(4)]),
+        "scat": (["offs", "val", "clear", "clear2"], lambda: [V.tensor_copy(T.posw[:].indirect(T.offs[:, 0:QE // 16]), T.vals[:])]),
         "turn": (["scat"], lambda: [V.transpose(T.trp[:], T.posw[:, 0:PT])]),
         "a1": (["da"], lambda: [V.tensor_scalar(T.a1[0:32, :], T.adS[0:32, :], 16.0 - nat0, None, Op.add)]),
         "a2": (["a1"], lambda: [V.tensor_scalar(T.a2[0:32, :], T.a1[0:32, :], 15, None, Op.bitwise_and)]),
@@ -291,48 +310,50 @@ def rank_program(g, core, T, topo):
     offsets(1)
     V.wait_ge(T.sem.dw, 128)
     S.wait_ge(T.sem.dw, 128)
-    e_q = []
-    for i in range(8):
-        a, sp, both = 1024 * i, CFG["split"] * width[i] // 1024, []
+    e_q, both = [], {}
+
+    def gather(i):
+        a, sp, both[i] = 1024 * i, CFG["split"][i], []
         if width[i]:
             m, n = sp // 16, width[i] // 16
             need("S", e_off[i])
-            both.append(sig(S.activation(T.ga[:, a:a + sp], T.win[:].indirect(T.offa[:, 64 * i:64 * i + m]), Fn.Copy)))
+            both[i].append(sig(S.activation(T.ga[:, a:a + sp], T.win[:].indirect(T.offa[:, 64 * i:64 * i + m]), Fn.Copy)))
             need("V", e_off[i])
-            both.append(sig(V.tensor_copy(T.ga[:, a + sp:a + width[i]], T.win[:].indirect(T.offa[:, 64 * i + m:64 * i + n]))))
+            both[i].append(sig(V.tensor_copy(T.ga[:, a + sp:a + width[i]], T.win[:].indirect(T.offa[:, 64 * i + m:64 * i + n]))))
             offsets(i + 2)
+
+    for i in range(CFG["lag"]):
+        gather(i)
+    for i in range(8):
+        a = 1024 * i
+        if i + CFG["lag"] < 8:
+            gather(i + CFG["lag"])
         work("V", CFG["fill"][i])
-        need("V", *both)
+        need("V", *both[i])
         if i == 7 and rows:
             V.wait_ge(T.sem.drow, 16 * rows)
         e_q.append(sig(V.quantize_mx(T.qc[:, 256 * i:256 * i + 256], T.qs[:, 256 * i:256 * i + 256], T.ga[:, a:a + 1024])))
     work("S", CFG["xS"][1])
     work("V", CFG["xV"])
 
-    held = {}
     for call in R["calls"]:
-        ts = []
-        for k, i, m, to, es in call:
-            need("g", *e_q[i:i + m])
-            if to is None:
-                dst, at, sem = cores[pairs[i]], 256 * rank, "a%d" % rank
-            else:
-                held[to] = held.get(to, -1) + 1
-                dst, at, sem = R["relay"][to], 256 * i, "h%d" % held[to]
-            ts.append(_tr(topo, dst, es, T.sem[sem], _run(T, BUFS[k][0], 256 * i, 256 * m), _run(T, BUFS[k][1], at, 256 * m)))
-            nloc += len(es)
-        g.remote_dma_fused(ts, local_sem=T.sem.loc)
+        need("g", *[e_q[i] for i, _es in call])
+        for k in R["pieces"][call[0][0], 0]:
+            g.remote_dma_fused([_hop(T, topo, rank, R, i, 0, k) for i, _es in call], local_sem=T.sem.loc)
+            nloc += sum(len(es) for _i, es in call)
     g.wait_ge(T.sem.loc, nloc)
 
     copies, last, n = [], {}, 0
     sender = {d: q for q in range(N) for d in roads[q]["who"] if roads[q]["who"][d] == rank}
-    for name in CFG["order"]:
+    for name in CFG["order"][R["h"]]:
         src = sender[name]
         if src == rank:
             need("P", e_q[7])
             cb, sb, at = T.qc, T.qs, 256 * 7
         else:
-            P.wait_ge(T.sem["a%d" % src], roads[src]["lands"][rank])
+            i = roads[src]["pairs"].index(rank)
+            hop = (i, len(roads[src]["road"][i]) - 2)
+            P.wait_ge(T.sem["a%d" % src], len(roads[src]["pieces"][hop]) * len(roads[src]["hops"][hop]))
             cb, sb, at = T.lc, T.ls, 256 * src
         for j in range(2):
             s, b = (2 * src + j - nat0) % 16, T["ps%d" % (n % 8)]
@@ -356,12 +377,13 @@ def rank_program(g, core, T, topo):
             n += 1
 
     need("V", ev["offy"], last["V"], last["S"])
-    e_y = sig(V.tensor_copy(T.ysb[:, 0:256], T.resw[:].indirect(T.offy[:, 0:16])))
     need("S", ev["offy"], last["S"], last["V"])
-    e_z = sig(S.activation(T.ysb[:, 256:512], T.resw[:].indirect(T.offy[:, 16:32]), Fn.Copy))
-    need("Y", e_y)
-    Y.dma_start(T.y[:, 0:256], T.ysb[:, 0:256]).then_inc(T.sem.dy0, 16)
-    need("S", e_z)
-    S.dma_start(T.y[:, 256:512], T.ysb[:, 256:512]).then_inc(T.sem.dy1, 16)
-    Y.wait_ge(T.sem.dy0, 16)
-    S.wait_ge(T.sem.dy1, 16)
+    done = {"Y": 0, "S": 0}
+    for qn, a, b, by in CFG["tail"]:
+        src = T.resw[:].indirect(T.offy[:, a // 16:b // 16])
+        need(by, sig(V.tensor_copy(T.ysb[:, a:b], src) if qn == "V" else S.activation(T.ysb[:, a:b], src, Fn.Copy)))
+        (Y if by == "Y" else S).dma_start(T.y[:, a:b], T.ysb[:, a:b]).then_inc(T.sem["dy0" if by == "Y" else "dy1"], 16)
+        done[by] += 16
+    Y.wait_ge(T.sem.dy0, done["Y"])
+    if done["S"]:
+        S.wait_ge(T.sem.dy1, done["S"])

from concourse.bass import DstId, RemoteDMATransfer, IndirectOffsetOnAxis
from concourse.mybir import dt, AluOpType as Op, ActivationFunctionType as Fn

NB = 10
NC = 128 * NB
NAT = 6
W0 = 512 * NAT
QE = NC // 4
PT = 544
CFG = {
    "split": [704, 672, 704, 672, 672, 608, 608, 0],
    "gate": (3, 6),
    "rows": 2,
    "groups": 2 * [[[("other", ["far", "mate0"]), ("ring", ["port"])], [("other0", ["mate1"]), ("plane0", ["near"])],
                    [("ring0", []), ("plane1", ["far"])], [("nb", [])]]],
    "first": 4 * ["sc"], "fine": "sc", "turns": True, "lag": 1,
    "order": 2 * [["me", "ring", "nb", "other0", "plane1", "other", "plane0", "ring0"]],
    "early": ["offx", "nd", "ramp", "o1", "c", "offs", "i0", "xq", "idx", "scat", "a1"],
    "fill": [[], [], [], [], [], ["a2"], ["t1"], ["t2", "turn"]],
    "xS": ([(0, 1024, 0), (0, 1024, 1)], [(0, 512, 2), (512, 1024, 2)] + [(1024, NC, _t) for _t in range(4)]),
    "xV": ["u", (0, 512, 3), "c1", (512, 1024, 3), "m1", (0, 512), "c2", (512, 1024), "m2", (1024, NC), "offy"],
    "copyV": (3, 5, 7, 9, 11, 13, 15),
    "tail": [("V", 0, 256, "Y"), ("S", 256, 512, "S")],
}

SCRATCH = {n: ("sbuf", [128, w], d) for d, ws in {
    "int32": {"tabo": 16, "tabb": 16, "tabc": 4, "tokS": 80, "adS": 32, "pidx": 4, "pi1": 4, "pi2": 4, "pi3": 4, "q1": 4,
              "q2": 4, "a1": 32, "a2": 32, "idx": 4},
    "bfloat16": {"rep": 32, "tabf": 32, "win": 4096, "xs": 2048, "xg": 4 * NC, "ga": 8192},
    "uint16": {"offa": 512, "offx": 80, "offs": 32, "offy": 32, "qoff": 4, "pick": 4, "zero": 4},
    "float32": {"p16": 4, "pf": 4, "ev16": 4, "b20": 4, "bq": 4, "bq4": 4, "i0": 4, "iot": QE // 4, "ramp": 32, "dump": 80, "nd": 80,
                "o1": 80, "vals": QE, "posw": PT + 8 * QE + 16, "trp": PT, "t1": 32, "t2": 32, "u": 32, "c1": 32,
                "m1": 32, "c2": 32, "m2": 32, "resw": W0 + NC, "ysb": 512},
    "float8_e4m3fn_x4": {"qc": 2048, "lc": 2048, "xc": 512, "xgc": NC},
    "uint8": {"qs": 2048, "ls": 2048, "xcs": 512, "xgs": NC},
}.items() for n, w in ws.items()}
SCRATCH["tabd"] = ("dram", [128, 1], "int32")
SCRATCH["tabr"] = ("dram", [8, 128, 1], "int32")
for _b in range(8):
    SCRATCH["ps%d" % _b] = ("psum", [128, 512], "float32")
SEMAPHORES = (["e%d" % _i for _i in range(126)] + ["a%d" % _i for _i in range(8)]
              + ["dtab", "down", "dtw", "dx", "dw", "dt", "da", "dy0", "dy1", "tabs", "tsent", "loc", "dto", "drow"])
BUFS = {"c": ("qc", "lc"), "s": ("qs", "ls")}
PIECES = {"s": (BUFS["s"], 0, 256), "c": (BUFS["c"], 0, 256), "a": (BUFS["c"], 0, 128), "b": (BUFS["c"], 128, 128)}
ALL_CORES = 128


def _mask(es):
    return sum(1 << e for e in es)


def _part(es, parts, k):
    n = len(es) // parts
    return es[n * k:n * k + n]


def _road(r, T, topo):
    cores = list(T.cores)
    n = len(cores)
    me = cores[r]
    on_chip = [q for q in range(n) if topo.chip(cores[q]) == topo.chip(me)]
    h = on_chip.index(r)
    nb = on_chip[1 - h]
    step = r - nb
    who = {"me": r, "nb": nb, "ring": (r + step) % n, "ring0": (r + 2 * step) % n, "plane1": (r + 3 * step) % n,
           "plane0": (r + 4 * step) % n, "other": (r + 5 * step) % n, "other0": (r + 6 * step) % n}
    groups = CFG["groups"][h]
    pairs = [who[d] for grp in groups for d, _way in grp]
    free = [c for c in topo.cores_of(me) if c not in cores]
    port = [c for c in free if topo.die(c) != topo.die(me) and topo.may_write(c, cores[who["ring"]])]
    local = {"port": port[h], "far": [c for c in free if topo.die(c) != topo.die(me) and c not in port][h],
             "near": [c for c in free if topo.die(c) == topo.die(me)][h]}

    def relay(v, d):
        if v in local:
            return local[v]
        k, hd = int(v[-1]), [c for c in cores if topo.chip(c) == topo.chip(d)].index(d)
        return [c for c in range(ALL_CORES) if topo.chip(c) != topo.chip(d) and topo.mates(topo.chip(c), topo.chip(d))
                and topo.may_write(c, d) and topo.die(c) == ((k + hd) % 2 if CFG["turns"] else k)][k if CFG["turns"] else hd]

    off = topo.engines(me, cores[who["ring"]])
    every = topo.engines(me, cores[nb])
    on = [e for e in every if e not in off]
    away = [q for q in range(n) if q not in on_chip]
    tab = {d: [off[i]] for i, d in enumerate(away)}
    tab[nb] = on[:1]
    road = [[me] + [relay(v, cores[who[d]]) for v in way] + [cores[who[d]]] for grp in groups for d, way in grp]
    calls, i = [], 0
    for grp in groups:
        ids, i = range(i, i + len(grp)), i + len(grp)
        out = [j for j in ids if topo.chip(road[j][1]) != topo.chip(me)]
        stay = [j for j in ids if j not in out]
        calls.append([(j, _part(off, len(out), out.index(j))) for j in out]
                     + [(j, _part(on if out or ids[0] else every, len(stay), stay.index(j))) for j in stay])
    hops = {}
    for j, es in sum(calls, []):
        hops[j, 0] = es
        for a in range(1, len(road[j]) - 1):
            hops[j, a] = topo.engines(road[j][a], road[j][a + 1])
    first = [ks for grp, ks in zip(groups, CFG["first"]) for _d in grp]
    pieces = {(j, a): CFG["fine"] if a and len(road[j]) > 3 else first[j] for j, a in hops}
    return {"who": who, "h": h, "pieces": pieces, "pairs": pairs, "tab": tab, "road": road, "calls": calls, "hops": hops}


def _tr(topo, dst, engines, sem, src, to):
    rid, pid, _se = topo.addr(dst)
    return RemoteDMATransfer(dst_ids=[DstId(rid=rid, pnc=pid)], dma_engine_mask=_mask(engines), remote_sem=sem, src=src, dst=to)


def _run(T, name, a, w):
    v = T[name][:, a:a + w]
    return v.bitcast(dt.uint8) if name in BUFS["c"] else v


def _held(k, i):
    return "e%d" % (len(PIECES) * i + list(PIECES).index(k))


def _hop(T, topo, r, R, i, a, k):
    last = a + 2 == len(R["road"][i])
    bufs, o, w = PIECES[k]
    return _tr(topo, R["road"][i][a + 1], R["hops"][i, a], T.sem["a%d" % r if last else _held(k, i)],
               _run(T, bufs[min(a, 1)], 256 * i + o, w), _run(T, bufs[1], 256 * (r if last else i) + o, w))


def _relay(g, core, r, R, T, topo):
    n = 0
    for i, road in enumerate(R["road"]):
        if core in road[1:-1]:
            a = road.index(core)
            for k in R["pieces"][i, a]:
                g.wait_ge(T.sem[_held(k if k in R["pieces"][i, a - 1] else "c", i)], len(R["hops"][i, a - 1]))
                g.remote_dma_fused([_hop(T, topo, r, R, i, a, k)], local_sem=T.sem.loc)
                n += len(R["hops"][i, a])
    if n:
        g.wait_ge(T.sem.loc, n)


def rank_program(g, core, T, topo):
    rank = T.rank_of(core)
    cores = list(T.cores)
    N = len(cores)
    roads = [_road(q, T, topo) for q in range(N)]
    if rank is None:
        for q, R in enumerate(roads):
            _relay(g, core, q, R, T, topo)
        return
    R = roads[rank]
    V, S, P, Y = g.vector, g.scalar, g.tensor, g.sync
    pairs = R["pairs"] + [rank]
    rows = CFG["rows"]
    nat0 = 2 * (rank - 1) % 16
    c0 = 8 * ((nat0 + NAT) % 16)
    used = [0]
    waited = {}

    def new():
        used[0] += 1
        return ["e%d" % (used[0] - 1), 0]

    def sig(inst, e=None):
        e = e or new()
        inst.then_inc(T.sem[e[0]], 1)
        e[1] += 1
        return e

    def need(qn, *es):
        q = {"g": g, "V": V, "S": S, "P": P, "Y": Y}[qn]
        for e in es:
            if waited.get((qn, e[0]), 0) < e[1]:
                q.wait_ge(T.sem[e[0]], e[1])
                waited[(qn, e[0])] = e[1]

    Y.dma_start(T.tabd[0:16, :], T.tab[:]).then_inc(T.sem.dtab, 16)
    S.dma_start(T.tabd[16:128, :], T.tok[0:7, 0:16]).then_inc(T.sem.dtab, 16)
    cut, w = min(80, 128 - c0), QE // 16
    runs = [(a, z) for a, z in ((0, cut), (cut, 80)) if a < z]
    for b, q in enumerate((S, Y)):
        for a, z in runs:
            q.dma_start(T.tokS[16 * b:16 * b + 16, a:z], T.tok[:, (c0 + a) % 128:(c0 + a) % 128 + z - a]).then_inc(T.sem.dt, 16)
    Y.dma_start(T.xs[:], T.x[:]).then_inc(T.sem.dx, 16)
    if rows:
        S.dma_start(T.tabo[0:1, 0:16], T.tab[:]).then_inc(T.sem.dto, 16)
    for b in range(2):
        S.dma_start(T.adS[16 * b:16 * b + 16, :], T.ad[:]).then_inc(T.sem.da, 16)
    S.dma_start(T.tabr[rank, 0:16, :], T.tab[:]).then_inc(T.sem.down, 16)

    def load(ms):
        for m in ms:
            Y.dma_start(T.win[:, 512 * m:512 * m + 512], T.wa[128 * m:128 * m + 128, :]).then_inc(T.sem.dw, 16)

    load(range(CFG["gate"][0]))
    Y.wait_ge(T.sem.tsent, 1)
    load(range(*CFG["gate"]))

    e_pidx = sig(g.iota(T.pidx[:, 0:1], [[0, 1]], 0, 1))
    e_dump = sig(g.iota(T.dump[0:32, :], [[-32, 80]], -PT, -1, allow_small_or_imprecise_dtypes=True))
    e_iot = sig(g.iota(T.iot[:], [[1, QE // 4]], 0, 0, allow_small_or_imprecise_dtypes=True))
    g.wait_ge(T.sem.dtab, 32)
    g.remote_dma_fused([_tr(topo, cores[d], R["tab"][d], T.sem.tabs, T.tabd[:], T.tabr[rank]) for d in pairs[:7]],
                       local_sem=T.sem.loc)
    nloc = sum(len(R["tab"][d]) for d in pairs[:7])
    g.sem_inc(T.sem.tsent, 1)
    ev = {"dt": ["dt", 32 * len(runs)], "da": ["da", 32], "dx": ["dx", 16]}
    if rows:
        g.wait_ge(T.sem.dto, 16)
        ev["pb"] = sig(g.partition_broadcast(T.tabb[:], T.tabo[0:1, 0:16], 128))

    e_z = sig(V.memset(T.tabc[:], 0))
    ev["z"] = sig(V.memset(T.t2[:], 0.0))
    sig(V.memset(T.zero[:], 0), ev["z"])
    need("V", e_pidx)
    e1 = sig(V.tensor_scalar(T.pi1[:, 0:1], T.pidx[:, 0:1], 15, None, Op.bitwise_and))
    sig(V.tensor_scalar(T.pi2[:, 0:1], T.pidx[:, 0:1], 16, None, Op.bitwise_and), e1)
    sig(V.tensor_scalar(T.pi3[:, 0:1], T.pidx[:, 0:1], 5, None, Op.logical_shift_right), e1)
    e2 = sig(V.tensor_copy(T.pf[:, 0:1], T.pidx[:, 0:1]))
    ev["clear"] = sig(V.memset(T.posw[:, 0:PT // 2], 0.0))
    need("V", e1)
    e_bq = sig(V.tensor_scalar(T.bq[:, 0:1], T.pi3[:, 0:1], float(QE), float(W0), Op.mult, Op.add))
    sig(V.tensor_copy(T.p16[:, 0:1], T.pi1[:, 0:1]), e2)
    sig(V.tensor_scalar(T.ev16[:, 0:1], T.pi2[:, 0:1], -1.0, 16.0, Op.mult, Op.add), e2)
    ev.update(iot=e_iot, col=e2, dump=e_dump)
    need("V", e_iot, e_bq)
    need("S", sig(V.tensor_scalar(T.bq4[:], T.iot[:, 0:4], 80.0, T.bq[:, 0:1], Op.mult, Op.add)))
    ev["val"] = new()
    for a in range(4):
        sig(S.activation(T.vals[:, 80 * a:80 * a + 80], T.iot[:], Fn.Identity, bias=T.bq4[:, a:a + 1]), ev["val"])
    need("S", ev["dx"])
    ev["clear2"] = sig(S.activation(T.posw[:, PT // 2:PT], T.xs[:, 0:PT // 2], Fn.Identity, scale=0.0))

    Y.wait_ge(T.sem.down, 16)
    need("Y", e_z)
    Y.wait_ge(T.sem.tabs, sum(len(roads[q]["tab"][rank]) for q in range(N) if q != rank))
    for b in range(4):
        Y.dma_start(T.tabc[32 * b:32 * b + 16, 0:1], T.tabr[:, 2 * rank:2 * rank + 2, 0]).then_inc(T.sem.dtw, 16)
    load(range(CFG["gate"][1], 8))

    steps = {
        "ramp": (["iot", "col"], lambda: [V.tensor_scalar(T.ramp[:], T.iot[:, 0:32], 16.0, T.p16[:, 0:1], Op.mult, Op.add)]),
        "c": (["ramp"], lambda: [V.tensor_scalar(T.pick[:, 0:2], T.ramp[:, 0:2], 16.0, T.ev16[:, 0:1], Op.mult, Op.add)]),
        "offx": (["dt"], lambda: [V.tensor_scalar(T.offx[32 * b:32 * b + 32, :], T.tokS[0:32, :], 0.0, 4.0, Op.max, Op.mult)
                                  for b in range(4)]),
        "xq": (["dx"], lambda: [V.quantize_mx(T.xc[:], T.xcs[:], T.xs[:])]),
        "i0": (["pb"], lambda: [V.tensor_scalar(T.i0[:, 0:2], T.tabb[:, 2 * rank:2 * rank + 2], 0.0, 128.0, Op.max, Op.mult)]),
        "idx": (["i0"], lambda: [V.tensor_scalar(T.idx[:, 0:2], T.i0[:, 0:2], T.pf[:, 0:1], None, Op.add)]),
        "nd": (["dt", "dump"], lambda: [V.tensor_tensor(T.nd[0:32, :], T.tokS[0:32, :], T.dump[0:32, :], Op.mult)]),
        "o1": (["nd"], lambda: [V.tensor_tensor(T.o1[0:32, :], T.tokS[0:32, :], T.nd[0:32, :], Op.max)]),
        "offs": (["o1", "col"], lambda: [V.tensor_scalar(T.offs[32 * b:32 * b + 32, 0:w], T.o1[0:32, w * b:w * b + w],
                                                         T.ev16[0:32, 0:1], None, Op.add) for b in range(4)]),
        "scat": (["offs", "val", "clear", "clear2"], lambda: [V.tensor_copy(T.posw[:].indirect(T.offs[:, 0:QE // 16]), T.vals[:])]),
        "turn": (["scat"], lambda: [V.transpose(T.trp[:], T.posw[:, 0:PT])]),
        "a1": (["da"], lambda: [V.tensor_scalar(T.a1[0:32, :], T.adS[0:32, :], 16.0 - nat0, None, Op.add)]),
        "a2": (["a1"], lambda: [V.tensor_scalar(T.a2[0:32, :], T.a1[0:32, :], 15, None, Op.bitwise_and)]),
        "t1": (["a2"], lambda: [V.tensor_scalar(T.t1[0:32, :], T.a2[0:32, :], -512.0, 512.0 * (NAT - 1), Op.mult, Op.add)]),
        "t2": (["t1", "z"], lambda: [V.tensor_tensor(T.t2[0:32, :], T.t1[0:32, :], T.ramp[0:32, :], Op.add)]),
        "u": (["turn", "t2", "c"], lambda: [V.tensor_tensor(T.u[:], T.trp[:].indirect(T.pick[:, 0:2]), T.t2[:], Op.max)]),
        "c1": (["u"], lambda: [V.tensor_copy(T.c1[0:64, :], T.u[64:128, :])]),
        "m1": (["c1"], lambda: [V.tensor_tensor(T.m1[0:64, :], T.u[0:64, :], T.c1[0:64, :], Op.max)]),
        "c2": (["m1"], lambda: [V.tensor_copy(T.c2[0:32, :], T.m1[32:64, :])]),
        "m2": (["c2"], lambda: [V.tensor_tensor(T.m2[0:32, :], T.m1[0:32, :], T.c2[0:32, :], Op.max)]),
        "offy": (["m2"], lambda: [V.tensor_copy(T.offy[32 * b:32 * b + 32, :], T.m2[0:32, :]) for b in range(4)]),
    }
    e_xg, e_gq = [], []

    def work(qn, jobs):
        for job in jobs:
            if job in steps:
                if rows or job not in ("i0", "idx"):
                    need("V", *[ev[d] for d in steps[job][0]])
                    ev[job] = new()
                    for inst in steps[job][1]():
                        sig(inst, ev[job])
                continue
            a, b = job[:2] if R["who"]["nb"] > rank else (NC - job[1], NC - job[0])
            if len(job) == 2:
                need("V", *[e for a0, b0, e in e_xg if a0 < b and a < b0])
                e_gq.append((a, b, sig(V.quantize_mx(T.xgc[:, a:b], T.xgs[:, a:b], T.xg[:, 4 * a:4 * b]))))
                continue
            t = job[2]
            need(qn, ev["dx"], ev["offx"])
            out, src = T.xg[:, 4 * a + t:4 * b:4], T.xs[:, t:2048].indirect(T.offx[:, a // 16:b // 16])
            e_xg.append((a, b, sig(S.activation(out, src, Fn.Copy) if qn == "S" else V.tensor_copy(out, src))))

    work("V", CFG["early"])
    work("S", CFG["xS"][0])
    if rows:
        need("g", ev["idx"])
        for j in range(2 - rows, 2):
            g.indirect_dma_start(T.ga[:, 7168 + 512 * j:7680 + 512 * j], None, T.wa[:],
                                 IndirectOffsetOnAxis(ap=T.idx[:, j:j + 1], axis=0), bounds_check=1023).then_inc(T.sem.drow, 16)

    V.wait_ge(T.sem.dtw, 64)
    need("V", e_z, ev["z"])
    e = sig(V.tensor_scalar(T.rep[:], T.tabc[:].indirect(T.zero[:, 0:2]), 0.0, 512.0, Op.max, Op.mult))
    need("V", e)
    e = sig(V.transpose(T.tabf[:], T.rep[:]))
    need("V", e)
    e_off = {}
    width = [1024] * 7 + [1024 - 512 * rows]

    def offsets(i):
        if i < 8 and width[i]:
            d, e = pairs[i], new()
            for j in range(width[i] // 512):
                sig(V.tensor_scalar(T.offa[:, 64 * i + 32 * j:64 * i + 32 * j + 32], T.ramp[:],
                                    T.tabf[:, 2 * d + j:2 * d + j + 1], None, Op.add), e)
            e_off[i] = e

    offsets(0)
    offsets(1)
    V.wait_ge(T.sem.dw, 128)
    S.wait_ge(T.sem.dw, 128)
    e_q, both = [], {}

    def gather(i):
        a, sp, both[i] = 1024 * i, CFG["split"][i], []
        if width[i]:
            m, n = sp // 16, width[i] // 16
            need("S", e_off[i])
            both[i].append(sig(S.activation(T.ga[:, a:a + sp], T.win[:].indirect(T.offa[:, 64 * i:64 * i + m]), Fn.Copy)))
            need("V", e_off[i])
            both[i].append(sig(V.tensor_copy(T.ga[:, a + sp:a + width[i]], T.win[:].indirect(T.offa[:, 64 * i + m:64 * i + n]))))
            offsets(i + 2)

    for i in range(CFG["lag"]):
        gather(i)
    for i in range(8):
        a = 1024 * i
        if i + CFG["lag"] < 8:
            gather(i + CFG["lag"])
        work("V", CFG["fill"][i])
        need("V", *both[i])
        if i == 7 and rows:
            V.wait_ge(T.sem.drow, 16 * rows)
        e_q.append(sig(V.quantize_mx(T.qc[:, 256 * i:256 * i + 256], T.qs[:, 256 * i:256 * i + 256], T.ga[:, a:a + 1024])))
    work("S", CFG["xS"][1])
    work("V", CFG["xV"])

    for call in R["calls"]:
        need("g", *[e_q[i] for i, _es in call])
        for k in R["pieces"][call[0][0], 0]:
            g.remote_dma_fused([_hop(T, topo, rank, R, i, 0, k) for i, _es in call], local_sem=T.sem.loc)
            nloc += sum(len(es) for _i, es in call)
    g.wait_ge(T.sem.loc, nloc)

    copies, last, n = [], {}, 0
    sender = {d: q for q in range(N) for d in roads[q]["who"] if roads[q]["who"][d] == rank}
    for name in CFG["order"][R["h"]]:
        src = sender[name]
        if src == rank:
            need("P", e_q[7])
            cb, sb, at = T.qc, T.qs, 256 * 7
        else:
            i = roads[src]["pairs"].index(rank)
            hop = (i, len(roads[src]["road"][i]) - 2)
            P.wait_ge(T.sem["a%d" % src], len(roads[src]["pieces"][hop]) * len(roads[src]["hops"][hop]))
            cb, sb, at = T.lc, T.ls, 256 * src
        for j in range(2):
            s, b = (2 * src + j - nat0) % 16, T["ps%d" % (n % 8)]
            if n >= 8:
                need("P", copies[n - 8])
            if s >= NAT:
                x0, w, xa, xb = 128 * (s - NAT), 128, T.xgc, T.xgs
                need("P", *[e for a, b0, e in e_gq if a <= x0 < b0])
                out = W0 + x0
            else:
                x0, w, xa, xb = 0, 512, T.xc, T.xcs
                need("P", ev["xq"])
                out = 512 * (NAT - 1 - s)
            e = sig(P.matmul_mx(b[:, 0:w], cb[:, at + 128 * j:at + 128 * j + 128], sb[:, at + 128 * j:at + 128 * j + 128],
                                xa[:, x0:x0 + w], xb[:, x0:x0 + w], True, True))
            qn = "V" if n in CFG["copyV"] else "S"
            need(qn, e)
            copies.append(sig(V.tensor_copy(T.resw[:, out:out + w], b[:, 0:w]) if qn == "V"
                              else S.activation(T.resw[:, out:out + w], b[:, 0:w], Fn.Copy)))
            last[qn] = copies[-1]
            n += 1

    need("V", ev["offy"], last["V"], last["S"])
    need("S", ev["offy"], last["S"], last["V"])
    done = {"Y": 0, "S": 0}
    for qn, a, b, by in CFG["tail"]:
        src = T.resw[:].indirect(T.offy[:, a // 16:b // 16])
        need(by, sig(V.tensor_copy(T.ysb[:, a:b], src) if qn == "V" else S.activation(T.ysb[:, a:b], src, Fn.Copy)))
        (Y if by == "Y" else S).dma_start(T.y[:, a:b], T.ysb[:, a:b]).then_inc(T.sem["dy0" if by == "Y" else "dy1"], 16)
        done[by] += 16
    Y.wait_ge(T.sem.dy0, done["Y"])
    if done["S"]:
        S.wait_ge(T.sem.dy1, done["S"])
